import numpy as np
import ml_dtypes


def mxq(x, axis, fmt="e4m3"):
    dtype, down = {"e4m3": (ml_dtypes.float8_e4m3fn, 7), "e5m2": (ml_dtypes.float8_e5m2, 14)}[fmt]
    v = np.moveaxis(np.asarray(x, np.float32).astype(ml_dtypes.bfloat16).astype(np.float64), axis, -1)
    blocks = v.reshape(v.shape[:-1] + (-1, 32))
    amax = np.abs(blocks).max(-1, keepdims=True)
    byte = np.maximum(np.where(amax > 0, np.frexp(amax)[1] - 1 + 127, 0) - down, 1)
    scale = np.exp2(byte - 127.0)
    codes = (blocks / scale).astype(np.float32).astype(dtype).astype(np.float64)
    return np.moveaxis((codes * scale).reshape(v.shape), -1, axis)


WIDE = False


def mx_kscale(k):
    if not WIDE:
        return np.ones(k)
    levels = np.array([10, -10, 5, -5, 0])
    if k % 512:
        return np.exp2(np.random.permutation(np.resize(levels, k // 32))).repeat(32)
    a = np.empty((k // 512, 16))
    for p in range(k // 512):
        a[p, :8] = np.random.permutation(np.resize(levels, 8))
        for g in range(8):
            far = levels[np.abs(levels - a[p, g]) >= 10]
            a[p, g + 8] = far[np.random.randint(len(far))]
    return np.exp2(a.ravel()).repeat(32)


BF16 = ml_dtypes.bfloat16


def bf(x):
    return np.asarray(x, np.float32).astype(BF16)


def f64(x):
    return np.asarray(x).astype(np.float64)


E2M1 = np.array([0.0, 0.5, 1.0, 1.5, 2.0, 3.0, 4.0, 6.0, -0.0, -0.5, -1.0, -1.5, -2.0, -3.0, -4.0, -6.0])


def pack_weight(w, fmt):
    k, n = w.shape
    w = f64(bf(w)).reshape(k // 32, 32, n)
    amax = np.abs(w).max(1)
    if fmt == "e4m3":
        byte = np.frexp(amax)[1] - 1 + 127 - 7
    else:
        mant, ex = np.frexp(amax / 6.0)
        byte = np.where(mant > 0.5, ex, ex - 1) + 127
    byte = np.clip(np.where(amax > 0, byte, 1), 1, 254)
    scaled = (w * np.exp2(127.0 - byte)[:, None, :]).reshape(k, n).astype(np.float32)
    by_word = np.ascontiguousarray(scaled.reshape(k // 512, 128, 4, n).transpose(0, 1, 3, 2))
    if fmt == "e4m3":
        words = by_word.astype(ml_dtypes.float8_e4m3fn).view(np.uint8)
    else:
        c = by_word.astype(ml_dtypes.float4_e2m1fn).view(np.uint8) & 0xF
        words = c[..., 0::2] | (c[..., 1::2] << 4)
    return np.ascontiguousarray(words), np.ascontiguousarray(byte.astype(np.uint8).reshape(k // 512, 16, n))


def unpack_weight(words, scales, fmt):
    g, p, n, _ = words.shape
    if fmt == "e4m3":
        vals = np.ascontiguousarray(words).view(ml_dtypes.float8_e4m3fn).astype(np.float64)
    else:
        nib = np.empty((g, p, n, 4), np.uint8)
        nib[..., 0::2] = words & 0xF
        nib[..., 1::2] = words >> 4
        vals = E2M1[nib]
    vals = vals * np.repeat(np.exp2(scales.astype(np.float64) - 127.0), 8, axis=1)[..., None]
    return vals.transpose(0, 1, 3, 2).reshape(g * 512, n)

def planes(Y):
    n, m = Y.shape
    b = f64(bf(Y)).reshape(n // 32, 32, m)
    amax = np.abs(b).max(1)
    byte = np.clip(np.where(amax > 0, np.frexp(amax)[1] - 1 + 127 - 7, 1), 1, 254)
    codes = (b * np.exp2(127.0 - byte)[:, None, :]).reshape(n, m).astype(np.float32).astype(ml_dtypes.float8_e4m3fn).view(np.uint8)
    words = codes.reshape(n // 512, 128, 4, m).transpose(0, 1, 3, 2)
    return np.ascontiguousarray(words), np.ascontiguousarray(byte.astype(np.uint8).reshape(n // 512, 16, m))


N, D, F, K, T = 1024, 512, 1024, 4, 256


def logsumexp(v, axis):
    m = v.max(axis=axis, keepdims=True)
    return m + np.log(np.sum(np.exp(v - m), axis=axis, keepdims=True))


def head(hq, w):
    wq = mxq(f64(w).reshape(F, K * T), 0, "e4m3")
    return (hq @ wq).reshape(N, K, T)


def setup_inputs():
    s, t = mx_kscale(D), mx_kscale(F)
    tw = t[:, None, None]
    x = bf(np.random.standard_normal((N, D)) * s)
    y = bf(np.random.standard_normal((N, T)))
    w1_words, w1_scales = pack_weight(np.random.standard_normal((D, F)) / np.sqrt(D) / s[:, None], "e4m3")
    return {
        "x": x,
        "y": y,
        "w1_words": w1_words,
        "w1_scales": w1_scales,
        "gain": bf((1.0 + 0.25 * np.random.standard_normal(F)) * t),
        "wp": bf(np.random.standard_normal((F, K, T)) * 1.5 / np.sqrt(F) / tw),
        "wm": bf(np.random.standard_normal((F, K, T)) * 1.5 / np.sqrt(F) / tw),
        "ws": bf(np.random.standard_normal((F, K, T)) * 0.5 / np.sqrt(F) / tw),
    }


def core(x, y, w1_words, w1_scales, gain, wp, wm, ws):
    h = f64(gain)[None, :] * np.tanh(mxq(f64(x), 1, "e4m3") @ unpack_weight(w1_words, w1_scales, "e4m3"))
    hq = mxq(h, 1, "e4m3")

    l = head(hq, wp)
    lp = l - logsumexp(l, 1)

    mu = head(hq, wm)

    sd = head(hq, ws)

    z = (f64(y)[:, None, :] - mu) * np.exp(-sd)
    q = lp - sd - 0.5 * np.square(z)

    half_log_two_pi = 0.5 * np.log(2.0 * np.pi)
    return half_log_two_pi - logsumexp(q, 1)[:, 0, :]


def reference(x, y, w1_words, w1_scales, gain, wp, wm, ws):
    R_out = core(x, y, w1_words, w1_scales, gain, wp, wm, ws)
    words, scales = planes(R_out)
    return R_out, words, scales

@@ -1,0 +1,776 @@
+from contextlib import ExitStack
+import math
+
+import concourse.mybir as mybir
+from concourse.masks import make_identity
+
+F32 = mybir.dt.float32
+BF16 = mybir.dt.bfloat16
+U32 = mybir.dt.uint32
+I32 = mybir.dt.int32
+U8 = mybir.dt.uint8
+FP8X4 = mybir.dt.float8_e4m3fn_x4
+ACT = mybir.ActivationFunctionType
+ALU = mybir.AluOpType
+AX = mybir.AxisListType
+
+N, D, F, K, T = 1024, 512, 1024, 4, 256
+FLOPS = 2 * N * D * F + 2 * N * F * 3 * K * T
+HALF_LOG_2PI = 0.5 * math.log(2.0 * math.pi)
+ROOT_HALF = math.sqrt(0.5)
+P = 128
+PS = {"S": 1, "M": 2, "L": 2, "R": 2, "sum": 1}
+HTAG = "SMRLMRLS"
+
+
+def tile_mixturedensitynetworkelementwisenll_x2_kernel(
+    tc, x, y, w1_words, w1_scales, gain, wp, wm, ws, out_0, out_1, out_2
+):
+    nc = tc.nc
+    with ExitStack() as ctx:
+        keep = ctx.enter_context(tc.tile_pool(name="keep", bufs=1))
+        work = ctx.enter_context(tc.tile_pool(name="work", bufs=3))
+        psum = ctx.enter_context(tc.psum_pool(name="psum", bufs=1))
+        ctx.enter_context(tc.manual_schedule())
+        ENG = {"V": nc.vector, "G": nc.gpsimd}
+
+        def bank(name, shape, tag):
+            return psum.tile(shape, F32, name=name, tag=tag, bufs=PS[tag])
+
+        dummy = keep.tile([P, 1], F32, name="dummy")
+        nc.vector.memset(dummy[:], 0.0)
+        nc.scalar.activation(out=dummy[:], in_=dummy[:], func=ACT.Exp)
+        ident = keep.tile([P, P], F32, name="ident")
+        make_identity(nc, ident[:])
+        w1s_raw = keep.tile([P, F], U8, name="w1s_raw", align_bytes=64)
+        nc.vector.memset(w1s_raw[:].bitcast(I32), 0)
+        for q in range(4):
+            nc.scalar.dma_start(
+                out=w1s_raw[32 * q : 32 * q + 4, :].bitcast(I32),
+                in_=w1_scales[0][4 * q : 4 * q + 4, :].bitcast(I32),
+            )
+        gain_sb = keep.tile([P, 2, 4], BF16, name="gain_sb")
+        nc.scalar.dma_start(out=gain_sb[:], in_=gain.rearrange("(f p t) -> p f t", f=2, t=4))
+
+        x_sb = [keep.tile([P, 4, D], BF16, name="x_sb%d" % g) for g in range(2)]
+        w1_raw = keep.tile([P, F], U32, name="w1_raw", align_bytes=64)
+        y_sb = keep.tile([P, 2, 4, T], BF16, name="y_sb")
+        w_hbm = {"s": ws, "m": wm, "p": wp}
+        w_raw = {(w, f): keep.tile([P, 4, K * T], BF16, name="w_raw_%s%d" % (w, f)) for w in "smp" for f in range(2)}
+
+        def load_x(g, a, b):
+            src = x[512 * g : 512 * g + 512, :].rearrange("(p j) d -> p j d", j=4)
+            nc.sync.dma_start(out=x_sb[g][:, a:b, :], in_=src[:, a:b, :])
+
+        def load_w(w, f):
+            src = w_hbm[w][512 * f : 512 * f + 512].rearrange("(p j) k t -> p j (k t)", j=4)
+            nc.sync.dma_start(out=w_raw[w, f][:], in_=src)
+
+        load_x(0, 0, 2)
+        load_x(0, 2, 4)
+        nc.sync.dma_start(out=w1_raw[:].bitcast(I32), in_=w1_words[0].rearrange("p n t -> p (n t)").bitcast(I32))
+        load_w("s", 0)
+        load_w("s", 1)
+        load_x(1, 0, 4)
+        nc.sync.dma_start(out=y_sb[:], in_=y.rearrange("(g p j) t -> p g j t", g=2, j=4))
+        load_w("m", 0)
+        load_w("m", 1)
+        load_w("p", 0)
+        load_w("p", 1)
+
+        def codes(name, n):
+            return keep.tile([P, n], U32, name=name + "c", align_bytes=64), keep.tile([P, n], U8, name=name + "s", align_bytes=64)
+
+        x_q = [codes("xq%d" % g, 512) for g in range(2)]
+        w1_q = codes("w1q", F)
+        h_q = {(g, f): codes("hq%d%d" % (g, f), 512) for g in range(2) for f in range(2)}
+        w_q = {(w, f, h): codes("wq%s%d%d" % (w, f, h), 512) for w in "smp" for f in range(2) for h in range(2)}
+
+        xts = {}
+        xgs = {}
+
+        def xt(g, b):
+            words = x_sb[g][:].rearrange("p j d -> p (j d)").bitcast(F32)
+            t = bank("xt", [P, 2, 2, P], "LR"[b])
+            xts[g, b] = t
+            for jj in range(2):
+                for u in range(2):
+                    j = 2 * b + jj
+                    nc.tensor.transpose(t[:, jj, u, :], words[:, 256 * j + u : 256 * (j + 1) : 2], ident[:])
+
+        def xc(g, b, eng):
+            if g not in xgs:
+                xgs[g] = work.tile([P, 2048], BF16, name="xg", tag="wi", align_bytes=64, bufs=7)
+            dst = xgs[g][:].bitcast(F32).rearrange("p (j r u) -> p j r u", j=4, u=2)[:, 2 * b : 2 * b + 2]
+            src = xts[g, b][:].rearrange("p j u r -> p j r u")
+            if eng == "S":
+                nc.scalar.copy(dst, src)
+            else:
+                nc.vector.tensor_copy(out=dst, in_=src)
+
+        def quant(q, cols, src):
+            nc.vector.quantize_mx(out=q[0][:, cols].bitcast(FP8X4), scales=q[1][:, cols], in_=src)
+
+        ALL = slice(0, 512)
+
+        def xq(g):
+            quant(x_q[g], ALL, xgs[g][:])
+
+        def w1s():
+            nc.vector.tensor_copy(
+                out=w1_q[1][:].rearrange("p (f t m) -> p f m t", f=2, t=4),
+                in_=w1s_raw[:].rearrange("p (f m t) -> p f m t", f=2, t=4),
+            )
+
+        def w1c():
+            nc.vector.tensor_copy(
+                out=w1_q[0][:].bitcast(I32).rearrange("p (f t m) -> p f t m", f=2, t=4),
+                in_=w1_raw[:].bitcast(I32).rearrange("p (f m t) -> p f t m", f=2, t=4),
+            )
+
+        def mx(out, a, acols, b, bcols, start, stop):
+            nc.tensor.matmul_mx(
+                out=out,
+                lhsT=a[0][:, acols].bitcast(FP8X4),
+                lhsT_scale=a[1][:, acols],
+                rhs=b[0][:, bcols].bitcast(FP8X4),
+                rhs_scale=b[1][:, bcols],
+                start=start,
+                stop=stop,
+            )
+
+        acc1 = {}
+        ths = {}
+        hb = {}
+
+        def hm(g, f, t):
+            acc1[g, f, t] = bank("acc1", [P, 512], HTAG[4 * f + t])
+            c = 4 * f + t
+            mx(acc1[g, f, t][:], w1_q, slice(c * P, c * P + P), x_q[g], ALL, True, True)
+
+        def th(g, f, t):
+            if (g, f) not in ths:
+                ths[g, f] = work.tile([P, 4, 512], F32, name="ths", bufs=2)
+            nc.scalar.activation(out=ths[g, f][:, t, :], in_=acc1[g, f, t][:], func=ACT.Tanh)
+
+        def hg(g, f):
+            h = work.tile([P, 512, 4], BF16, name="h", tag="wi", align_bytes=64, bufs=7)
+            nc.vector.tensor_tensor(
+                out=h[:],
+                in0=ths[g, f][:].rearrange("p t n -> p n t"),
+                in1=gain_sb[:, f, :].unsqueeze(1).to_broadcast([P, 512, 4]),
+                op=ALU.mult,
+            )
+            hb[g, f] = h
+
+        def hq(g, f):
+            quant(h_q[g, f], ALL, hb[g, f][:].rearrange("p n t -> p (n t)"))
+
+        wi = {}
+
+        def inter(w, f, h, k, eng):
+            if (w, f, h) not in wi:
+                wi[w, f, h] = work.tile([P, 512, 4], BF16, name="wi", tag="wi", align_bytes=64, bufs=7)
+            ks = k if w is None else slice(k[0], k[1])
+            src = w_raw[w, f][:].rearrange("p j (k h t) -> p h k t j", k=4, h=2)[:, h, ks]
+            dst = wi[w, f, h][:].rearrange("p (k t) j -> p k t j", k=4)[:, ks]
+            sign = -1.0 if w == "s" else 1.0
+            if eng == "S":
+                nc.scalar.activation(out=dst, in_=src, func=ACT.Copy, scale=sign)
+            elif eng == "V":
+                nc.vector.tensor_scalar(out=dst, in0=src, scalar1=sign, scalar2=None, op0=ALU.mult)
+            else:
+                nc.gpsimd.tensor_scalar(out=dst, in0=src, scalar1=sign, scalar2=0.0, op0=ALU.mult, op1=ALU.add)
+
+        def wq(w, f, h):
+            quant(w_q[w, f, h], ALL, wi[w, f, h][:].rearrange("p c j -> p (c j)"))
+
+        units = [(h, g, j) for h in range(2) for g in range(2) for j in range(4)]
+        ab = [keep.tile([P, 2, 4, P], F32, name="ab%d" % b) for b in range(4)]
+        mxs = [keep.tile([P, 2, 4, P], F32, name="mx%d" % b) for b in range(4)]
+        osp = [keep.tile([P, T], U8, name="os%d" % g, align_bytes=64) for g in range(2)]
+        acc = {}
+        dt = {}
+        et = {}
+        xx = {}
+        sb = {}
+        SUMJ = {}
+        ot = {}
+
+        def mm(u, tag, names):
+            h, g, j = units[u]
+            a = bank("acc" + tag, [P, 4, P], tag)
+            acc[u, tag] = a
+            passes = [(w, f) for w in names for f in range(2)]
+            for i, (w, f) in enumerate(passes):
+                mx(
+                    a[:].rearrange("p k t -> p (k t)"),
+                    h_q[g, f],
+                    slice(j * P, j * P + P),
+                    w_q[w, f, h],
+                    ALL,
+                    i == 0,
+                    i == len(passes) - 1,
+                )
+
+        def mS(u):
+            mm(u, "S", "s")
+
+        def mM(u):
+            mm(u, "M", "m")
+
+        def mL(u):
+            mm(u, "L", "p")
+
+        def mR(u):
+            mm(u, "R", "ps")
+
+        def wide(ap):
+            return ap.unsqueeze(1).to_broadcast([P, 4, P])
+
+        def e(u):
+            et[u] = work.tile([P, 4, P], F32, name="et", bufs=3)
+            nc.scalar.activation(out=et[u][:], in_=acc[u, "S"][:], func=ACT.Exp)
+
+        def d(u):
+            h, g, j = units[u]
+            dt[u] = work.tile([P, 4, P], F32, name="dt", bufs=5)
+            nc.vector.tensor_tensor(
+                out=dt[u][:], in0=acc[u, "M"][:], in1=wide(y_sb[:, g, j, h * P : h * P + P]), op=ALU.subtract
+            )
+
+        def z(u):
+            nc.gpsimd.tensor_tensor(out=dt[u][:], in0=dt[u][:], in1=et[u][:], op=ALU.mult)
+
+        def sq(u):
+            nc.scalar.activation(out=dt[u][:], in_=dt[u][:], func=ACT.Square, scale=ROOT_HALF)
+
+        def ml(u):
+            nc.vector.tensor_reduce(
+                out=mxs[u // 4][:, 0, u % 4, :], in_=acc[u, "L"][:].rearrange("p k t -> p t k"), axis=AX.X, op=ALU.max
+            )
+
+        def ld(u):
+            xx[u] = work.tile([P, 2, 4, P], F32, name="xx", bufs=5)
+            nc.vector.tensor_tensor(
+                out=xx[u][:, 0], in0=acc[u, "L"][:], in1=wide(mxs[u // 4][:, 0, u % 4, :]), op=ALU.subtract
+            )
+
+        def q(u):
+            nc.vector.tensor_tensor(out=dt[u][:], in0=acc[u, "R"][:], in1=dt[u][:], op=ALU.subtract)
+
+        def mq(u):
+            nc.vector.tensor_reduce(
+                out=mxs[u // 4][:, 1, u % 4, :], in_=dt[u][:].rearrange("p k t -> p t k"), axis=AX.X, op=ALU.max
+            )
+
+        def qd(u, eng="V"):
+            ENG[eng].tensor_tensor(
+                out=xx[u][:, 1], in0=dt[u][:], in1=wide(mxs[u // 4][:, 1, u % 4, :]), op=ALU.subtract
+            )
+
+        def p(u):
+            nc.scalar.activation(out=xx[u][:], in_=xx[u][:], func=ACT.Exp)
+
+        def ts(u):
+            b, j = u // 4, u % 4
+            if b not in sb:
+                sb[b] = bank("sb", [P, 4, P], "sum")
+            SUMJ.setdefault(b, []).append(j)
+            for k in range(4):
+                nc.tensor.matmul(out=sb[b][:, j, :], lhsT=ident[:], rhs=xx[u][:, 1, k, :], start=(k == 0), stop=(k == 3))
+
+        st1 = {}
+
+        def s1(u, whats, eng):
+            st1[u] = work.tile([P, 2, 2, P], F32, name="s1", bufs=2)
+            ENG[eng].tensor_tensor(
+                out=st1[u][:, whats], in0=xx[u][:, whats, 0:2], in1=xx[u][:, whats, 2:4], op=ALU.add
+            )
+
+        def s2(u, whats, eng):
+            ENG[eng].tensor_tensor(
+                out=ab[u // 4][:, whats, u % 4, :], in0=st1[u][:, whats, 0], in1=st1[u][:, whats, 1], op=ALU.add
+            )
+
+        def sc(b):
+            a = SUMJ[b][0]
+            for i, j in enumerate(SUMJ[b]):
+                if i + 1 == len(SUMJ[b]) or SUMJ[b][i + 1] != j + 1:
+                    nc.scalar.copy(ab[b][:, 1, a : j + 1, :], sb[b][:, a : j + 1, :])
+                    a = SUMJ[b][i + 1] if i + 1 < len(SUMJ[b]) else 0
+
+        def fd(b, eng="G"):
+            ENG[eng].tensor_tensor(out=mxs[b][:, 0], in0=mxs[b][:, 0], in1=mxs[b][:, 1], op=ALU.subtract)
+
+        def flat(t):
+            return t[:].rearrange("p a j t -> p (a j t)")
+
+        def la(b):
+            nc.scalar.activation(out=flat(ab[b])[:, 0:896], in_=flat(ab[b])[:, 0:896], func=ACT.Ln)
+
+        def ln(b):
+            c = 896 if b == 3 else 0
+            nc.scalar.activation(out=flat(ab[b])[:, c:1024], in_=flat(ab[b])[:, c:1024], func=ACT.Ln)
+
+        def t1(b, eng="G"):
+            ENG[eng].tensor_tensor(out=mxs[b][:, 0], in0=mxs[b][:, 0], in1=ab[b][:, 0], op=ALU.add)
+
+        def opart(b, js):
+            if b not in ot:
+                ot[b] = work.tile([P, 4, P], F32, name="o", bufs=2)
+            nc.vector.scalar_tensor_tensor(
+                out=ot[b][:, js],
+                in0=mxs[b][:, 0, js],
+                scalar=HALF_LOG_2PI,
+                in1=ab[b][:, 1, js],
+                op0=ALU.add,
+                op1=ALU.subtract,
+            )
+
+        def oa(b):
+            opart(b, slice(0, 3))
+
+        def o(b):
+            h, g = b // 2, b % 2
+            opart(b, slice(3, 4) if b == 3 else slice(0, 4))
+            v = ot[b]
+            nc.sync.dma_start(
+                out=out_0[512 * g : 512 * g + 512, h * P : h * P + P].rearrange("(p j) t -> p j t", j=4), in_=v[:]
+            )
+
+        obt = {}
+
+        def ob(b, eng):
+            obt[b] = work.tile([P, P, 4], BF16, name="ob", bufs=1, align_bytes=64)
+            src = ot[b][:].rearrange("p j t -> p t j")
+            if eng == "S":
+                nc.scalar.copy(obt[b][:], src)
+            else:
+                nc.vector.tensor_copy(out=obt[b][:], in_=src)
+
+        def oq(b):
+            h, g = b // 2, b % 2
+            cols = slice(h * P, h * P + P)
+            oc = work.tile([P, P], U32, name="oc", bufs=1, align_bytes=64)
+            nc.vector.quantize_mx(
+                out=oc[:].bitcast(FP8X4), scales=osp[g][:, cols], in_=obt[b][:].rearrange("p t j -> p (t j)")
+            )
+            nc.sync.dma_start(
+                out=out_1[g][:, cols, :].rearrange("p m b -> p (m b)").bitcast(I32), in_=oc[:].bitcast(I32)
+            )
+            if h == 1:
+                for qq in range(4):
+                    nc.sync.dma_start(
+                        out=out_2[g][4 * qq : 4 * qq + 4, :].bitcast(I32),
+                        in_=osp[g][32 * qq : 32 * qq + 4, :].bitcast(I32),
+                    )
+
+        xt(0, 0)
+        xt(0, 1)
+        xc(0, 0, "S")
+        xc(0, 1, "S")
+        w1s()
+        w1c()
+        xq(0)
+        hm(0, 1, 0)
+        hm(0, 1, 1)
+        inter("s", 0, 1, (0, 1), "V")
+        th(0, 1, 0)
+        hm(0, 1, 2)
+        inter("s", 0, 0, (2, 3), "V")
+        hm(0, 1, 3)
+        inter("s", 0, 0, (1, 2), "S")
+        inter("s", 0, 0, (0, 1), "V")
+        hm(0, 0, 1)
+        hm(0, 0, 2)
+        inter("s", 0, 1, (1, 2), "G")
+        th(0, 1, 1)
+        hm(0, 0, 3)
+        inter("s", 0, 1, (2, 3), "G")
+        th(0, 1, 2)
+        th(0, 1, 3)
+        inter("s", 1, 0, (0, 1), "V")
+        inter("s", 1, 0, (1, 2), "V")
+        inter("s", 0, 0, (3, 4), "S")
+        hm(0, 0, 0)
+        hg(0, 1)
+        xt(1, 0)
+        th(0, 0, 0)
+        xt(1, 1)
+        xc(1, 0, "S")
+        th(0, 0, 1)
+        wq("s", 0, 0)
+        th(0, 0, 2)
+        th(0, 0, 3)
+        hq(0, 1)
+        xc(1, 1, "S")
+        hg(0, 0)
+        inter("m", 0, 0, (3, 4), "S")
+        inter("m", 0, 0, (0, 1), "S")
+        inter("m", 0, 0, (1, 2), "S")
+        xq(1)
+        inter("s", 0, 1, (3, 4), "S")
+        hq(0, 0)
+        hm(1, 1, 1)
+        inter("s", 1, 0, (3, 4), "S")
+        hm(1, 1, 2)
+        wq("s", 0, 1)
+        hm(1, 1, 0)
+        hm(1, 1, 3)
+        th(1, 1, 0)
+        inter("m", 0, 0, (2, 3), "G")
+        hm(1, 0, 1)
+        hm(1, 0, 2)
+        inter("m", 1, 0, (1, 2), "S")
+        hm(1, 0, 3)
+        inter("m", 1, 0, (0, 1), "V")
+        inter("m", 1, 0, (3, 4), "V")
+        inter("m", 1, 0, (2, 3), "S")
+        inter("p", 0, 0, (1, 2), "V")
+        inter("p", 0, 0, (0, 1), "V")
+        th(1, 1, 1)
+        wq("m", 1, 0)
+        th(1, 1, 2)
+        wq("m", 0, 0)
+        th(1, 1, 3)
+        inter("s", 1, 0, (2, 3), "G")
+        mM(0)
+        inter("p", 0, 0, (3, 4), "S")
+        hm(1, 0, 0)
+        wq("s", 1, 0)
+        inter("p", 0, 0, (2, 3), "S")
+        d(0)
+        inter("p", 1, 0, (0, 1), "G")
+        inter("p", 1, 0, (2, 3), "S")
+        inter("m", 1, 1, (0, 1), "V")
+        inter("p", 1, 0, (3, 4), "S")
+        inter("p", 0, 1, (2, 3), "V")
+        inter("p", 1, 0, (1, 2), "S")
+        hg(1, 1)
+        th(1, 0, 0)
+        inter("m", 0, 1, (1, 2), "S")
+        mS(0)
+        e(0)
+        wq("p", 1, 0)
+        th(1, 0, 1)
+        mS(1)
+        wq("p", 0, 0)
+        th(1, 0, 2)
+        mM(1)
+        hq(1, 1)
+        e(1)
+        mM(2)
+        z(0)
+        d(1)
+        th(1, 0, 3)
+        mS(2)
+        d(2)
+        inter("s", 1, 1, (0, 1), "S")
+        mL(0)
+        hg(1, 0)
+        e(2)
+        mR(0)
+        sq(0)
+        inter("s", 1, 1, (2, 3), "S")
+        mS(3)
+        mL(1)
+        inter("s", 1, 1, (3, 4), "S")
+        q(0)
+        z(1)
+        mM(3)
+        e(3)
+        ml(0)
+        mR(1)
+        inter("m", 0, 1, (0, 1), "S")
+        hq(1, 0)
+        sq(1)
+        ld(0)
+        z(2)
+        mR(2)
+        inter("m", 0, 1, (3, 4), "S")
+        mq(0)
+        q(1)
+        qd(0, "G")
+        sq(2)
+        mL(2)
+        d(3)
+        inter("s", 1, 1, (1, 2), "S")
+        mS(4)
+        q(2)
+        z(3)
+        mM(4)
+        p(0)
+        ml(1)
+        mM(5)
+        ml(2)
+        mR(3)
+        e(4)
+        s1(0, slice(0, 2), "G")
+        ld(1)
+        sq(3)
+        ld(2)
+        mS(5)
+        inter("p", 0, 1, (0, 1), "S")
+        wq("s", 1, 1)
+        mL(3)
+        e(5)
+        s2(0, slice(0, 2), "G")
+        mq(1)
+        mL(4)
+        inter("m", 1, 1, (1, 2), "S")
+        mq(2)
+        inter("p", 0, 1, (1, 2), "G")
+        mS(6)
+        inter("m", 0, 1, (2, 3), "S")
+        ml(3)
+        inter("p", 1, 1, (0, 1), "G")
+        mR(4)
+        d(4)
+        e(6)
+        qd(1, "V")
+        inter("m", 1, 1, (2, 3), "S")
+        mS(7)
+        qd(2, "V")
+        p(1)
+        mM(6)
+        z(4)
+        d(5)
+        d(6)
+        p(2)
+        ts(1)
+        ld(3)
+        s1(1, slice(0, 1), "G")
+        ml(4)
+        e(7)
+        s1(2, slice(0, 1), "G")
+        ts(2)
+        q(3)
+        sq(4)
+        z(5)
+        ld(4)
+        inter("m", 1, 1, (3, 4), "S")
+        mS(8)
+        q(4)
+        inter("p", 0, 1, (3, 4), "S")
+        mL(5)
+        z(6)
+        mq(3)
+        mL(6)
+        e(8)
+        ml(5)
+        sq(5)
+        mS(9)
+        ml(6)
+        fd(0, "G")
+        sq(6)
+        mM(7)
+        ld(5)
+        e(9)
+        mR(5)
+        ld(6)
+        s2(1, slice(0, 1), "G")
+        inter("p", 1, 1, (2, 3), "S")
+        s2(2, slice(0, 1), "G")
+        mq(4)
+        inter("p", 1, 1, (1, 2), "S")
+        mS(10)
+        wq("p", 0, 1)
+        mR(6)
+        inter("p", 1, 1, (3, 4), "S")
+        wq("m", 0, 1)
+        qd(3, "V")
+        mL(7)
+        qd(4, "G")
+        q(5)
+        p(3)
+        q(6)
+        mR(7)
+        wq("p", 1, 1)
+        p(4)
+        ts(3)
+        wq("m", 1, 1)
+        s1(3, slice(0, 1), "G")
+        mq(5)
+        mM(8)
+        mq(6)
+        sc(0)
+        s1(4, slice(0, 1), "G")
+        mL(8)
+        d(7)
+        qd(6, "G")
+        ts(4)
+        d(8)
+        ml(7)
+        z(7)
+        ml(8)
+        mM(9)
+        ld(7)
+        mM(10)
+        z(8)
+        d(9)
+        e(10)
+        mL(9)
+        ld(8)
+        sq(7)
+        mS(11)
+        qd(5, "V")
+        sq(8)
+        mL(10)
+        q(7)
+        z(9)
+        p(5)
+        mR(8)
+        ml(9)
+        mq(7)
+        s2(3, slice(0, 1), "G")
+        p(6)
+        ts(5)
+        ld(9)
+        s1(5, slice(0, 1), "G")
+        q(8)
+        ln(0)
+        s2(4, slice(0, 1), "G")
+        mR(9)
+        d(10)
+        s2(5, slice(0, 1), "G")
+        fd(1, "G")
+        mq(8)
+        mM(11)
+        ml(10)
+        mM(12)
+        s1(6, slice(0, 2), "V")
+        mR(10)
+        qd(7, "V")
+        sq(9)
+        qd(8, "V")
+        p(7)
+        mL(11)
+        q(9)
+        z(10)
+        ld(10)
+        mR(11)
+        s2(6, slice(0, 2), "V")
+        mq(9)
+        t1(0, "G")
+        mL(12)
+        d(11)
+        e(11)
+        ts(7)
+        d(12)
+        s1(7, slice(0, 1), "G")
+        p(8)
+        ml(11)
+        z(11)
+        mS(12)
+        ml(12)
+        sq(10)
+        mM(13)
+        ld(11)
+        e(12)
+        s1(8, slice(0, 1), "G")
+        mM(14)
+        ld(12)
+        sc(1)
+        mS(13)
+        z(12)
+        q(10)
+        sq(11)
+        ts(8)
+        d(13)
+        e(13)
+        qd(9, "V")
+        sq(12)
+        mS(14)
+        z(13)
+        d(14)
+        p(9)
+        mM(15)
+        mq(10)
+        mL(13)
+        s2(7, slice(0, 1), "G")
+        q(11)
+        e(14)
+        mR(12)
+        s2(8, slice(0, 1), "G")
+        ml(13)
+        sq(13)
+        z(14)
+        mq(11)
+        ln(1)
+        mS(15)
+        q(12)
+        mL(14)
+        fd(2, "G")
+        ld(13)
+        mR(13)
+        mq(12)
+        qd(11, "G")
+        ml(14)
+        mL(15)
+        q(13)
+        e(15)
+        mR(14)
+        s1(9, slice(0, 2), "V")
+        qd(10, "V")
+        mR(15)
+        t1(1, "G")
+        d(15)
+        p(10)
+        ml(15)
+        z(15)
+        ld(14)
+        sq(14)
+        mq(13)
+        ts(10)
+        p(11)
+        o(1)
+        qd(12, "V")
+        sq(15)
+        ts(11)
+        s1(10, slice(0, 1), "G")
+        q(14)
+        p(12)
+        q(15)
+        s2(10, slice(0, 1), "G")
+        ld(15)
+        sc(2)
+        s2(9, slice(0, 2), "V")
+        qd(13, "V")
+        ob(1, "S")
+        ts(12)
+        s1(11, slice(0, 1), "G")
+        mq(14)
+        p(13)
+        oq(1)
+        s1(12, slice(0, 1), "G")
+        mq(15)
+        sc(3)
+        qd(14, "V")
+        qd(15, "V")
+        p(14)
+        o(0)
+        fd(3, "G")
+        p(15)
+        ob(0, "S")
+        s2(11, slice(0, 1), "G")
+        s2(12, slice(0, 1), "G")
+        ln(2)
+        s1(13, slice(0, 2), "V")
+        s1(14, slice(0, 2), "V")
+        s2(13, slice(0, 2), "V")
+        s1(15, slice(0, 2), "V")
+        s2(14, slice(0, 2), "V")
+        s2(15, slice(0, 2), "V")
+        t1(2, "V")
+        la(3)
+        oq(0)
+        o(2)
+        t1(3, "V")
+        ln(3)
+        ob(2, "V")
+        oa(3)
+        oq(2)
+        o(3)
+        ob(3, "V")
+        oq(3)

@@ -239,8 +239,8 @@ def tile_mixturedensitynetworkelementwisenll_x2_kernel(
                 out=dt[u][:], in0=acc[u, "M"][:], in1=wide(y_sb[:, g, j, h * P : h * P + P]), op=ALU.subtract
             )
 
-        def z(u):
-            nc.gpsimd.tensor_tensor(out=dt[u][:], in0=dt[u][:], in1=et[u][:], op=ALU.mult)
+        def z(u, eng="G"):
+            ENG[eng].tensor_tensor(out=dt[u][:], in0=dt[u][:], in1=et[u][:], op=ALU.mult)
 
         def sq(u):
             nc.scalar.activation(out=dt[u][:], in_=dt[u][:], func=ACT.Square, scale=ROOT_HALF)
@@ -366,409 +366,409 @@ def tile_mixturedensitynetworkelementwisenll_x2_kernel(
                         in_=osp[g][32 * qq : 32 * qq + 4, :].bitcast(I32),
                     )
 
+        w1s()
         xt(0, 0)
         xt(0, 1)
         xc(0, 0, "S")
         xc(0, 1, "S")
-        w1s()
         w1c()
         xq(0)
         hm(0, 1, 0)
         hm(0, 1, 1)
-        inter("s", 0, 1, (0, 1), "V")
         th(0, 1, 0)
         hm(0, 1, 2)
-        inter("s", 0, 0, (2, 3), "V")
+        inter("s", 0, 0, (1, 2), "V")
         hm(0, 1, 3)
-        inter("s", 0, 0, (1, 2), "S")
-        inter("s", 0, 0, (0, 1), "V")
+        inter("s", 0, 0, (0, 1), "S")
         hm(0, 0, 1)
+        inter("s", 0, 0, (2, 3), "V")
         hm(0, 0, 2)
-        inter("s", 0, 1, (1, 2), "G")
-        th(0, 1, 1)
+        inter("s", 0, 0, (3, 4), "V")
         hm(0, 0, 3)
-        inter("s", 0, 1, (2, 3), "G")
+        th(0, 1, 1)
+        wq("s", 0, 0)
         th(0, 1, 2)
         th(0, 1, 3)
-        inter("s", 1, 0, (0, 1), "V")
-        inter("s", 1, 0, (1, 2), "V")
-        inter("s", 0, 0, (3, 4), "S")
+        inter("s", 1, 1, (0, 1), "V")
+        inter("s", 1, 1, (1, 2), "V")
+        inter("s", 1, 1, (3, 4), "S")
         hm(0, 0, 0)
         hg(0, 1)
         xt(1, 0)
         th(0, 0, 0)
         xt(1, 1)
         xc(1, 0, "S")
-        th(0, 0, 1)
-        wq("s", 0, 0)
-        th(0, 0, 2)
-        th(0, 0, 3)
-        hq(0, 1)
         xc(1, 1, "S")
-        hg(0, 0)
-        inter("m", 0, 0, (3, 4), "S")
-        inter("m", 0, 0, (0, 1), "S")
-        inter("m", 0, 0, (1, 2), "S")
+        inter("s", 1, 1, (2, 3), "V")
+        th(0, 0, 1)
         xq(1)
-        inter("s", 0, 1, (3, 4), "S")
-        hq(0, 0)
-        hm(1, 1, 1)
-        inter("s", 1, 0, (3, 4), "S")
-        hm(1, 1, 2)
-        wq("s", 0, 1)
+        th(0, 0, 2)
+        wq("s", 1, 1)
         hm(1, 1, 0)
+        th(0, 0, 3)
+        hm(1, 1, 1)
+        inter("m", 0, 0, (1, 2), "V")
         hm(1, 1, 3)
-        th(1, 1, 0)
-        inter("m", 0, 0, (2, 3), "G")
+        inter("m", 0, 0, (0, 1), "S")
+        inter("m", 0, 0, (2, 3), "V")
+        hm(1, 1, 2)
+        inter("m", 0, 0, (3, 4), "V")
         hm(1, 0, 1)
+        th(1, 1, 0)
+        hg(0, 0)
         hm(1, 0, 2)
-        inter("m", 1, 0, (1, 2), "S")
         hm(1, 0, 3)
-        inter("m", 1, 0, (0, 1), "V")
-        inter("m", 1, 0, (3, 4), "V")
+        inter("s", 1, 0, (1, 2), "S")
+        inter("m", 1, 0, (0, 1), "S")
+        inter("m", 1, 0, (1, 2), "S")
+        inter("s", 1, 0, (0, 1), "V")
         inter("m", 1, 0, (2, 3), "S")
-        inter("p", 0, 0, (1, 2), "V")
-        inter("p", 0, 0, (0, 1), "V")
+        inter("s", 1, 0, (3, 4), "V")
+        hq(0, 1)
         th(1, 1, 1)
-        wq("m", 1, 0)
+        inter("p", 0, 0, (1, 2), "V")
         th(1, 1, 2)
-        wq("m", 0, 0)
+        inter("p", 0, 0, (3, 4), "V")
+        hq(0, 0)
         th(1, 1, 3)
-        inter("s", 1, 0, (2, 3), "G")
-        mM(0)
-        inter("p", 0, 0, (3, 4), "S")
+        inter("s", 1, 0, (2, 3), "S")
+        wq("m", 0, 0)
         hm(1, 0, 0)
-        wq("s", 1, 0)
-        inter("p", 0, 0, (2, 3), "S")
-        d(0)
-        inter("p", 1, 0, (0, 1), "G")
-        inter("p", 1, 0, (2, 3), "S")
-        inter("m", 1, 1, (0, 1), "V")
-        inter("p", 1, 0, (3, 4), "S")
-        inter("p", 0, 1, (2, 3), "V")
-        inter("p", 1, 0, (1, 2), "S")
         hg(1, 1)
         th(1, 0, 0)
-        inter("m", 0, 1, (1, 2), "S")
-        mS(0)
-        e(0)
-        wq("p", 1, 0)
+        inter("p", 0, 0, (0, 1), "S")
         th(1, 0, 1)
-        mS(1)
-        wq("p", 0, 0)
         th(1, 0, 2)
-        mM(1)
-        hq(1, 1)
-        e(1)
-        mM(2)
-        z(0)
-        d(1)
+        wq("s", 1, 0)
         th(1, 0, 3)
-        mS(2)
-        d(2)
-        inter("s", 1, 1, (0, 1), "S")
-        mL(0)
+        hq(1, 1)
+        mS(0)
+        inter("p", 0, 0, (2, 3), "S")
+        inter("p", 1, 0, (1, 2), "V")
         hg(1, 0)
-        e(2)
-        mR(0)
-        sq(0)
-        inter("s", 1, 1, (2, 3), "S")
-        mS(3)
-        mL(1)
-        inter("s", 1, 1, (3, 4), "S")
-        q(0)
-        z(1)
-        mM(3)
-        e(3)
-        ml(0)
-        mR(1)
-        inter("m", 0, 1, (0, 1), "S")
+        inter("p", 1, 0, (0, 1), "S")
+        inter("p", 1, 0, (2, 3), "S")
+        inter("p", 1, 0, (3, 4), "S")
+        e(0)
+        wq("p", 0, 0)
+        inter("p", 1, 1, (0, 1), "S")
+        wq("p", 1, 0)
+        mS(1)
+        inter("p", 1, 1, (1, 2), "S")
         hq(1, 0)
-        sq(1)
-        ld(0)
-        z(2)
-        mR(2)
-        inter("m", 0, 1, (3, 4), "S")
-        mq(0)
-        q(1)
-        qd(0, "G")
-        sq(2)
-        mL(2)
-        d(3)
-        inter("s", 1, 1, (1, 2), "S")
-        mS(4)
-        q(2)
-        z(3)
-        mM(4)
-        p(0)
+        mL(0)
+        e(1)
+        inter("m", 1, 1, (2, 3), "V")
+        mL(1)
+        ml(0)
+        inter("p", 1, 1, (3, 4), "S")
+        inter("m", 1, 0, (3, 4), "G")
+        mR(0)
         ml(1)
-        mM(5)
+        inter("m", 1, 1, (0, 1), "S")
+        inter("p", 1, 1, (2, 3), "G")
+        ld(0)
+        inter("m", 1, 1, (1, 2), "S")
+        mR(1)
+        ld(1)
+        inter("m", 1, 1, (3, 4), "S")
+        wq("p", 1, 1)
+        mL(2)
+        wq("m", 1, 0)
+        mL(3)
         ml(2)
+        inter("p", 0, 1, (0, 1), "S")
+        inter("p", 0, 1, (3, 4), "G")
+        mM(0)
+        ml(3)
+        mM(1)
+        inter("p", 0, 1, (1, 2), "S")
+        inter("m", 0, 1, (3, 4), "G")
+        d(0)
+        mS(2)
+        inter("p", 0, 1, (2, 3), "S")
+        d(1)
+        mM(2)
+        e(2)
+        z(0, "V")
+        mM(3)
+        inter("m", 0, 1, (0, 1), "S")
+        d(2)
+        mS(3)
+        z(1, "G")
+        d(3)
+        sq(0)
+        mM(4)
+        ld(2)
+        e(3)
+        mM(5)
+        z(2, "G")
+        q(0)
+        sq(1)
+        mL(4)
+        d(4)
+        inter("m", 0, 1, (1, 2), "S")
+        mS(4)
+        q(1)
+        z(3, "G")
+        mM(6)
+        sq(2)
+        mq(0)
+        mR(2)
+        inter("m", 0, 1, (2, 3), "S")
+        mq(1)
+        qd(0, "G")
+        sq(3)
+        ld(3)
         mR(3)
         e(4)
-        s1(0, slice(0, 2), "G")
-        ld(1)
-        sq(3)
-        ld(2)
-        mS(5)
-        inter("p", 0, 1, (0, 1), "S")
-        wq("s", 1, 1)
-        mL(3)
-        e(5)
-        s2(0, slice(0, 2), "G")
-        mq(1)
-        mL(4)
-        inter("m", 1, 1, (1, 2), "S")
-        mq(2)
-        inter("p", 0, 1, (1, 2), "G")
-        mS(6)
-        inter("m", 0, 1, (2, 3), "S")
-        ml(3)
-        inter("p", 1, 1, (0, 1), "G")
-        mR(4)
-        d(4)
-        e(6)
-        qd(1, "V")
-        inter("m", 1, 1, (2, 3), "S")
-        mS(7)
-        qd(2, "V")
-        p(1)
-        mM(6)
-        z(4)
-        d(5)
-        d(6)
-        p(2)
-        ts(1)
-        ld(3)
-        s1(1, slice(0, 1), "G")
-        ml(4)
-        e(7)
-        s1(2, slice(0, 1), "G")
-        ts(2)
-        q(3)
-        sq(4)
-        z(5)
-        ld(4)
-        inter("m", 1, 1, (3, 4), "S")
-        mS(8)
-        q(4)
-        inter("p", 0, 1, (3, 4), "S")
-        mL(5)
-        z(6)
-        mq(3)
-        mL(6)
-        e(8)
-        ml(5)
-        sq(5)
-        mS(9)
-        ml(6)
-        fd(0, "G")
-        sq(6)
-        mM(7)
-        ld(5)
-        e(9)
-        mR(5)
-        ld(6)
-        s2(1, slice(0, 1), "G")
-        inter("p", 1, 1, (2, 3), "S")
-        s2(2, slice(0, 1), "G")
-        mq(4)
-        inter("p", 1, 1, (1, 2), "S")
-        mS(10)
-        wq("p", 0, 1)
-        mR(6)
-        inter("p", 1, 1, (3, 4), "S")
+        q(2)
+        inter("s", 0, 1, (0, 1), "S")
         wq("m", 0, 1)
-        qd(3, "V")
+        mL(5)
+        p(0)
+        qd(1, "V")
+        mS(5)
+        d(5)
+        mR(4)
+        z(4, "G")
+        p(1)
+        d(6)
+        q(3)
+        mM(7)
+        e(5)
+        s1(0, slice(0, 1), "G")
+        mq(2)
+        ts(0)
+        sq(4)
+        mq(3)
+        s1(1, slice(0, 2), "G")
+        inter("s", 0, 1, (1, 2), "S")
+        q(4)
+        mS(6)
+        sc(0)
+        ml(4)
+        s2(0, slice(0, 1), "G")
+        mR(5)
+        e(6)
+        ml(5)
+        s2(1, slice(0, 2), "G")
+        inter("s", 0, 1, (2, 3), "S")
+        ld(4)
+        mS(7)
+        z(5, "G")
+        inter("s", 0, 1, (3, 4), "S")
+        ld(5)
+        mL(6)
+        mq(4)
+        e(7)
         mL(7)
+        fd(0, "G")
+        ml(6)
+        sq(5)
+        mR(6)
+        ml(7)
         qd(4, "G")
         q(5)
-        p(3)
-        q(6)
+        ld(6)
         mR(7)
-        wq("p", 1, 1)
-        p(4)
-        ts(3)
-        wq("m", 1, 1)
-        s1(3, slice(0, 1), "G")
         mq(5)
-        mM(8)
-        mq(6)
-        sc(0)
-        s1(4, slice(0, 1), "G")
-        mL(8)
-        d(7)
-        qd(6, "G")
-        ts(4)
-        d(8)
-        ml(7)
-        z(7)
-        ml(8)
-        mM(9)
-        ld(7)
-        mM(10)
-        z(8)
-        d(9)
-        e(10)
-        mL(9)
-        ld(8)
-        sq(7)
-        mS(11)
+        wq("s", 0, 1)
+        qd(2, "V")
+        mS(8)
         qd(5, "V")
-        sq(8)
-        mL(10)
-        q(7)
-        z(9)
+        p(2)
+        d(7)
+        qd(3, "V")
+        e(8)
+        z(6, "V")
+        p(3)
+        mS(9)
+        wq("p", 0, 1)
+        wq("m", 1, 1)
+        sq(6)
+        mL(8)
+        s1(3, slice(0, 2), "V")
+        p(4)
+        mM(8)
+        q(6)
+        mM(9)
+        s1(2, slice(0, 2), "G")
+        d(8)
         p(5)
         mR(8)
-        ml(9)
-        mq(7)
-        s2(3, slice(0, 1), "G")
-        p(6)
-        ts(5)
-        ld(9)
-        s1(5, slice(0, 1), "G")
-        q(8)
-        ln(0)
-        s2(4, slice(0, 1), "G")
-        mR(9)
-        d(10)
-        s2(5, slice(0, 1), "G")
-        fd(1, "G")
-        mq(8)
+        mq(6)
+        z(7, "G")
+        ld(7)
+        e(9)
+        mM(10)
+        ml(8)
+        mL(9)
+        s2(2, slice(0, 2), "G")
+        d(9)
+        sq(7)
+        mS(10)
+        ld(8)
+        z(8, "G")
         mM(11)
-        ml(10)
+        e(10)
+        q(7)
+        mL(10)
+        d(10)
+        z(9, "G")
+        mS(11)
+        sq(8)
+        mq(7)
         mM(12)
-        s1(6, slice(0, 2), "V")
-        mR(10)
-        qd(7, "V")
+        e(11)
+        ml(9)
+        ts(4)
+        fd(1, "G")
+        q(8)
         sq(9)
+        ml(10)
+        mS(12)
+        mq(8)
+        z(10, "G")
+        mR(9)
+        e(12)
+        mS(13)
+        s2(3, slice(0, 2), "V")
+        sq(10)
+        qd(6, "V")
+        mR(10)
+        ln(0)
+        qd(7, "V")
         qd(8, "V")
+        s1(5, slice(0, 2), "V")
+        d(11)
+        s1(4, slice(0, 1), "G")
+        d(12)
+        p(6)
+        mM(13)
+        z(11, "G")
+        q(9)
+        mM(14)
+        d(13)
+        mR(11)
+        q(10)
+        s2(4, slice(0, 1), "G")
+        z(12, "G")
+        ld(9)
+        mM(15)
+        ld(10)
         p(7)
         mL(11)
-        q(9)
-        z(10)
-        ld(10)
-        mR(11)
-        s2(6, slice(0, 2), "V")
         mq(9)
-        t1(0, "G")
         mL(12)
-        d(11)
-        e(11)
-        ts(7)
-        d(12)
-        s1(7, slice(0, 1), "G")
+        s2(5, slice(0, 2), "V")
         p(8)
-        ml(11)
-        z(11)
-        mS(12)
-        ml(12)
-        sq(10)
-        mM(13)
-        ld(11)
-        e(12)
-        s1(8, slice(0, 1), "G")
-        mM(14)
-        ld(12)
-        sc(1)
-        mS(13)
-        z(12)
-        q(10)
-        sq(11)
-        ts(8)
-        d(13)
-        e(13)
+        ts(6)
         qd(9, "V")
-        sq(12)
-        mS(14)
-        z(13)
+        s1(7, slice(0, 2), "V")
+        e(13)
+        s1(8, slice(0, 1), "V")
+        mR(12)
+        s2(7, slice(0, 2), "V")
+        sc(1)
+        s2(8, slice(0, 1), "V")
         d(14)
-        p(9)
-        mM(15)
-        mq(10)
-        mL(13)
-        s2(7, slice(0, 1), "G")
+        sq(11)
+        s1(6, slice(0, 1), "G")
+        mS(14)
+        ml(11)
+        sq(12)
+        ts(8)
+        z(13, "G")
         q(11)
         e(14)
-        mR(12)
-        s2(8, slice(0, 1), "G")
-        ml(13)
-        sq(13)
-        z(14)
-        mq(11)
-        ln(1)
-        mS(15)
         q(12)
-        mL(14)
-        fd(2, "G")
-        ld(13)
+        p(9)
+        mS(15)
+        ld(11)
+        s2(6, slice(0, 1), "G")
+        z(14, "G")
         mR(13)
-        mq(12)
-        qd(11, "G")
-        ml(14)
-        mL(15)
-        q(13)
+        ml(12)
+        sq(13)
+        mq(10)
         e(15)
-        mR(14)
-        s1(9, slice(0, 2), "V")
-        qd(10, "V")
-        mR(15)
-        t1(1, "G")
-        d(15)
-        p(10)
-        ml(15)
-        z(15)
-        ld(14)
+        mL(13)
+        ld(12)
+        qd(10, "G")
         sq(14)
-        mq(13)
-        ts(10)
-        p(11)
-        o(1)
-        qd(12, "V")
-        sq(15)
-        ts(11)
-        s1(10, slice(0, 1), "G")
+        mR(14)
+        q(13)
+        ln(1)
+        ml(13)
+        s1(9, slice(0, 1), "G")
+        mL(14)
+        d(15)
+        mR(15)
         q(14)
-        p(12)
+        s2(9, slice(0, 1), "G")
+        ld(13)
+        z(15, "G")
+        ts(9)
+        ml(14)
+        p(10)
+        mq(11)
+        t1(1, "G")
+        mL(15)
+        mq(12)
+        ld(14)
+        fd(2, "G")
+        mq(13)
+        mq(14)
+        sq(15)
+        ts(10)
+        s1(10, slice(0, 1), "G")
+        ml(15)
         q(15)
         s2(10, slice(0, 1), "G")
         ld(15)
         sc(2)
-        s2(9, slice(0, 2), "V")
+        qd(11, "V")
+        qd(12, "V")
+        p(11)
         qd(13, "V")
-        ob(1, "S")
-        ts(12)
-        s1(11, slice(0, 1), "G")
-        mq(14)
-        p(13)
-        oq(1)
-        s1(12, slice(0, 1), "G")
-        mq(15)
-        sc(3)
         qd(14, "V")
+        p(12)
+        s1(11, slice(0, 2), "V")
+        mq(15)
+        p(13)
+        ts(12)
+        s2(11, slice(0, 2), "V")
         qd(15, "V")
         p(14)
-        o(0)
-        fd(3, "G")
+        s1(12, slice(0, 1), "V")
+        s1(13, slice(0, 1), "V")
+        ts(13)
+        s2(12, slice(0, 1), "V")
+        s2(13, slice(0, 1), "V")
+        t1(0, "V")
         p(15)
-        ob(0, "S")
-        s2(11, slice(0, 1), "G")
-        s2(12, slice(0, 1), "G")
+        s1(14, slice(0, 1), "V")
+        ts(14)
+        o(0)
         ln(2)
-        s1(13, slice(0, 2), "V")
-        s1(14, slice(0, 2), "V")
-        s2(13, slice(0, 2), "V")
-        s1(15, slice(0, 2), "V")
-        s2(14, slice(0, 2), "V")
-        s2(15, slice(0, 2), "V")
+        s2(14, slice(0, 1), "V")
+        s1(15, slice(0, 1), "V")
+        ob(0, "V")
+        ts(15)
+        s2(15, slice(0, 1), "V")
+        oq(0)
+        o(1)
+        fd(3, "G")
+        ob(1, "S")
+        sc(3)
+        oq(1)
         t1(2, "V")
         la(3)
-        oq(0)
         o(2)
-        t1(3, "V")
         ln(3)
-        ob(2, "V")
+        t1(3, "V")
+        ob(2, "S")
         oa(3)
         oq(2)
         o(3)

@@ -52,8 +52,13 @@ def tile_mixturedensitynetworkelementwisenll_x2_kernel(
         gain_sb = keep.tile([P, 2, 4], BF16, name="gain_sb")
         nc.scalar.dma_start(out=gain_sb[:], in_=gain.rearrange("(f p t) -> p f t", f=2, t=4))
 
-        x_sb = [keep.tile([P, 4, D], BF16, name="x_sb%d" % g) for g in range(2)]
-        w1_raw = keep.tile([P, F], U32, name="w1_raw", align_bytes=64)
+        def ring(shape, dtype, name):
+            return work.tile(shape, dtype, name=name, tag="wi", align_bytes=64, bufs=8)
+
+        x_sb0 = ring([P, 4, D], BF16, "x_sb0")
+        w1_raw = ring([P, F], U32, "w1_raw")
+        x_sb1 = ring([P, 4, D], BF16, "x_sb1")
+        x_sb = [x_sb0, x_sb1]
         y_sb = keep.tile([P, 2, 4, T], BF16, name="y_sb")
         w_hbm = {"s": ws, "m": wm, "p": wp}
         w_raw = {(w, f): keep.tile([P, 4, K * T], BF16, name="w_raw_%s%d" % (w, f)) for w in "smp" for f in range(2)}
@@ -100,7 +105,7 @@ def tile_mixturedensitynetworkelementwisenll_x2_kernel(
 
         def xc(g, b, eng):
             if g not in xgs:
-                xgs[g] = work.tile([P, 2048], BF16, name="xg", tag="wi", align_bytes=64, bufs=7)
+                xgs[g] = ring([P, 2048], BF16, "xg")
             dst = xgs[g][:].bitcast(F32).rearrange("p (j r u) -> p j r u", j=4, u=2)[:, 2 * b : 2 * b + 2]
             src = xts[g, b][:].rearrange("p j u r -> p j r u")
             if eng == "S":
@@ -153,12 +158,12 @@ def tile_mixturedensitynetworkelementwisenll_x2_kernel(
                 ths[g, f] = work.tile([P, 4, 512], F32, name="ths", bufs=2)
             nc.scalar.activation(out=ths[g, f][:, t, :], in_=acc1[g, f, t][:], func=ACT.Tanh)
 
-        def hg(g, f):
-            h = work.tile([P, 512, 4], BF16, name="h", tag="wi", align_bytes=64, bufs=7)
-            nc.vector.tensor_tensor(
-                out=h[:],
-                in0=ths[g, f][:].rearrange("p t n -> p n t"),
-                in1=gain_sb[:, f, :].unsqueeze(1).to_broadcast([P, 512, 4]),
+        def hg(g, f, eng="V"):
+            h = ring([P, 512, 4], BF16, "h")
+            ENG[eng].tensor_tensor(
+                out=h[:].rearrange("p (c i) t -> p c t i", i=4),
+                in0=ths[g, f][:].rearrange("p t (c i) -> p c t i", i=4),
+                in1=gain_sb[:, f, :].unsqueeze(1).unsqueeze(3).to_broadcast([P, 128, 4, 4]),
                 op=ALU.mult,
             )
             hb[g, f] = h
@@ -170,13 +175,15 @@ def tile_mixturedensitynetworkelementwisenll_x2_kernel(
 
         def inter(w, f, h, k, eng):
             if (w, f, h) not in wi:
-                wi[w, f, h] = work.tile([P, 512, 4], BF16, name="wi", tag="wi", align_bytes=64, bufs=7)
+                wi[w, f, h] = ring([P, 512, 4], BF16, "wi")
             ks = k if w is None else slice(k[0], k[1])
             src = w_raw[w, f][:].rearrange("p j (k h t) -> p h k t j", k=4, h=2)[:, h, ks]
             dst = wi[w, f, h][:].rearrange("p (k t) j -> p k t j", k=4)[:, ks]
             sign = -1.0 if w == "s" else 1.0
-            if eng == "S":
+            if eng == "S" and w == "s":
                 nc.scalar.activation(out=dst, in_=src, func=ACT.Copy, scale=sign)
+            elif eng == "S":
+                nc.scalar.copy(dst, src)
             elif eng == "V":
                 nc.vector.tensor_scalar(out=dst, in0=src, scalar1=sign, scalar2=None, op0=ALU.mult)
             else:
@@ -228,22 +235,28 @@ def tile_mixturedensitynetworkelementwisenll_x2_kernel(
         def wide(ap):
             return ap.unsqueeze(1).to_broadcast([P, 4, P])
 
+        def get(d, k, shape, name, bufs, tag=None):
+            if k not in d:
+                t = work.tile(shape, F32, name=name, tag=tag or name, bufs=bufs)
+                d[k] = t
+            return d[k]
+
         def e(u):
-            et[u] = work.tile([P, 4, P], F32, name="et", bufs=3)
-            nc.scalar.activation(out=et[u][:], in_=acc[u, "S"][:], func=ACT.Exp)
+            t = get(et, u // 2, [P, 2, 4, P], "et", 2)
+            nc.scalar.activation(out=t[:, u % 2], in_=acc[u, "S"][:], func=ACT.Exp)
 
         def d(u):
             h, g, j = units[u]
-            dt[u] = work.tile([P, 4, P], F32, name="dt", bufs=5)
+            t = get(dt, u // 2, [P, 2, 4, P], "dt", 3)
             nc.vector.tensor_tensor(
-                out=dt[u][:], in0=acc[u, "M"][:], in1=wide(y_sb[:, g, j, h * P : h * P + P]), op=ALU.subtract
+                out=t[:, u % 2], in0=acc[u, "M"][:], in1=wide(y_sb[:, g, j, h * P : h * P + P]), op=ALU.subtract
             )
 
-        def z(u, eng="G"):
-            ENG[eng].tensor_tensor(out=dt[u][:], in0=dt[u][:], in1=et[u][:], op=ALU.mult)
+        def z(v, eng):
+            ENG[eng].tensor_tensor(out=dt[v][:], in0=dt[v][:], in1=et[v][:], op=ALU.mult)
 
-        def sq(u):
-            nc.scalar.activation(out=dt[u][:], in_=dt[u][:], func=ACT.Square, scale=ROOT_HALF)
+        def sq(v):
+            nc.scalar.activation(out=dt[v][:], in_=dt[v][:], func=ACT.Square, scale=ROOT_HALF)
 
         def ml(u):
             nc.vector.tensor_reduce(
@@ -251,54 +264,76 @@ def tile_mixturedensitynetworkelementwisenll_x2_kernel(
             )
 
         def ld(u):
-            xx[u] = work.tile([P, 2, 4, P], F32, name="xx", bufs=5)
+            t = get(xx, u // 2, [P, 2, 2, 4, P], "xx", 3)
             nc.vector.tensor_tensor(
-                out=xx[u][:, 0], in0=acc[u, "L"][:], in1=wide(mxs[u // 4][:, 0, u % 4, :]), op=ALU.subtract
+                out=t[:, 0, u % 2], in0=acc[u, "L"][:], in1=wide(mxs[u // 4][:, 0, u % 4, :]), op=ALU.subtract
             )
 
         def q(u):
-            nc.vector.tensor_tensor(out=dt[u][:], in0=acc[u, "R"][:], in1=dt[u][:], op=ALU.subtract)
+            nc.vector.tensor_tensor(
+                out=dt[u // 2][:, u % 2], in0=acc[u, "R"][:], in1=dt[u // 2][:, u % 2], op=ALU.subtract
+            )
 
-        def mq(u):
+        m1 = {}
+
+        def pair(v):
+            return v // 2, slice(2 * (v % 2), 2 * (v % 2) + 2)
+
+        def mqa(v):
+            t = get(m1, v, [P, 2, 2, P], "m1", 1)
+            nc.vector.tensor_tensor(out=t[:], in0=dt[v][:, :, 0:2], in1=dt[v][:, :, 2:4], op=ALU.max)
+
+        def mqr(v):
+            b, js = pair(v)
             nc.vector.tensor_reduce(
-                out=mxs[u // 4][:, 1, u % 4, :], in_=dt[u][:].rearrange("p k t -> p t k"), axis=AX.X, op=ALU.max
+                out=mxs[b][:, 1, js, :], in_=dt[v][:].rearrange("p a k t -> p a t k"), axis=AX.X, op=ALU.max
             )
 
-        def qd(u, eng="V"):
+        def mqb(v):
+            b, js = pair(v)
+            nc.vector.tensor_tensor(out=mxs[b][:, 1, js, :], in0=m1[v][:, :, 0], in1=m1[v][:, :, 1], op=ALU.max)
+
+        def qd(v, eng):
+            b, js = pair(v)
+            t = get(xx, v, [P, 2, 2, 4, P], "xx", 3)
             ENG[eng].tensor_tensor(
-                out=xx[u][:, 1], in0=dt[u][:], in1=wide(mxs[u // 4][:, 1, u % 4, :]), op=ALU.subtract
+                out=t[:, 1],
+                in0=dt[v][:],
+                in1=mxs[b][:, 1, js, :].unsqueeze(2).to_broadcast([P, 2, 4, P]),
+                op=ALU.subtract,
             )
 
-        def p(u):
-            nc.scalar.activation(out=xx[u][:], in_=xx[u][:], func=ACT.Exp)
+        def pe(v, a):
+            nc.scalar.activation(out=xx[v][:, a], in_=xx[v][:, a], func=ACT.Exp)
 
-        def ts(u):
-            b, j = u // 4, u % 4
-            if b not in sb:
-                sb[b] = bank("sb", [P, 4, P], "sum")
-            SUMJ.setdefault(b, []).append(j)
+        def tsum(v, a):
+            t = sb.get(v)
+            if t is None:
+                t = bank("sb", [P, 2, 2, P], "sum")
+                sb[v] = t
+                SUMJ[v] = []
+            SUMJ[v].append(a)
             for k in range(4):
-                nc.tensor.matmul(out=sb[b][:, j, :], lhsT=ident[:], rhs=xx[u][:, 1, k, :], start=(k == 0), stop=(k == 3))
+                nc.tensor.matmul(out=t[:, a], lhsT=ident[:], rhs=xx[v][:, a, :, k, :], start=(k == 0), stop=(k == 3))
+
+        def cp(v):
+            b, js = pair(v)
+            if len(SUMJ[v]) == 2:
+                nc.scalar.copy(ab[b][:, :, js, :], sb[v][:])
+            else:
+                a = SUMJ[v][0]
+                nc.scalar.copy(ab[b][:, a, js, :], sb[v][:, a])
 
         st1 = {}
 
-        def s1(u, whats, eng):
-            st1[u] = work.tile([P, 2, 2, P], F32, name="s1", bufs=2)
-            ENG[eng].tensor_tensor(
-                out=st1[u][:, whats], in0=xx[u][:, whats, 0:2], in1=xx[u][:, whats, 2:4], op=ALU.add
-            )
+        def s1(v, a, eng):
+            t = get(st1, (v, a), [P, 2, 2, P], "s1", 1)
+            ENG[eng].tensor_tensor(out=t[:], in0=xx[v][:, a, :, 0:2], in1=xx[v][:, a, :, 2:4], op=ALU.add)
 
-        def s2(u, whats, eng):
-            ENG[eng].tensor_tensor(
-                out=ab[u // 4][:, whats, u % 4, :], in0=st1[u][:, whats, 0], in1=st1[u][:, whats, 1], op=ALU.add
-            )
-
-        def sc(b):
-            a = SUMJ[b][0]
-            for i, j in enumerate(SUMJ[b]):
-                if i + 1 == len(SUMJ[b]) or SUMJ[b][i + 1] != j + 1:
-                    nc.scalar.copy(ab[b][:, 1, a : j + 1, :], sb[b][:, a : j + 1, :])
-                    a = SUMJ[b][i + 1] if i + 1 < len(SUMJ[b]) else 0
+        def s2(v, a, eng):
+            b, js = pair(v)
+            t = st1[v, a]
+            ENG[eng].tensor_tensor(out=ab[b][:, a, js, :], in0=t[:, :, 0], in1=t[:, :, 1], op=ALU.add)
 
         def fd(b, eng="G"):
             ENG[eng].tensor_tensor(out=mxs[b][:, 0], in0=mxs[b][:, 0], in1=mxs[b][:, 1], op=ALU.subtract)
@@ -307,10 +342,10 @@ def tile_mixturedensitynetworkelementwisenll_x2_kernel(
             return t[:].rearrange("p a j t -> p (a j t)")
 
         def la(b):
-            nc.scalar.activation(out=flat(ab[b])[:, 0:896], in_=flat(ab[b])[:, 0:896], func=ACT.Ln)
+            nc.scalar.activation(out=flat(ab[b])[:, 0:768], in_=flat(ab[b])[:, 0:768], func=ACT.Ln)
 
         def ln(b):
-            c = 896 if b == 3 else 0
+            c = 768 if b == 3 else 0
             nc.scalar.activation(out=flat(ab[b])[:, c:1024], in_=flat(ab[b])[:, c:1024], func=ACT.Ln)
 
         def t1(b, eng="G"):
@@ -329,11 +364,11 @@ def tile_mixturedensitynetworkelementwisenll_x2_kernel(
             )
 
         def oa(b):
-            opart(b, slice(0, 3))
+            opart(b, slice(0, 2))
 
         def o(b):
             h, g = b // 2, b % 2
-            opart(b, slice(3, 4) if b == 3 else slice(0, 4))
+            opart(b, slice(2, 4) if b == 3 else slice(0, 4))
             v = ot[b]
             nc.sync.dma_start(
                 out=out_0[512 * g : 512 * g + 512, h * P : h * P + P].rearrange("(p j) t -> p j t", j=4), in_=v[:]
@@ -343,11 +378,12 @@ def tile_mixturedensitynetworkelementwisenll_x2_kernel(
 
         def ob(b, eng):
             obt[b] = work.tile([P, P, 4], BF16, name="ob", bufs=1, align_bytes=64)
-            src = ot[b][:].rearrange("p j t -> p t j")
+            src = ot[b][:].rearrange("p j (c i) -> p c j i", i=4)
+            dst = obt[b][:].rearrange("p (c i) j -> p c j i", i=4)
             if eng == "S":
-                nc.scalar.copy(obt[b][:], src)
+                nc.scalar.copy(dst, src)
             else:
-                nc.vector.tensor_copy(out=obt[b][:], in_=src)
+                nc.vector.tensor_copy(out=dst, in_=src)
 
         def oq(b):
             h, g = b // 2, b % 2
@@ -373,404 +409,332 @@ def tile_mixturedensitynetworkelementwisenll_x2_kernel(
         xc(0, 1, "S")
         w1c()
         xq(0)
+        hm(0, 0, 0)
+        hm(0, 0, 1)
+        th(0, 0, 0)
+        hm(0, 0, 2)
+        inter("s", 0, 1, (0, 2), "V")
+        hm(0, 0, 3)
+        inter("s", 0, 0, (2, 4), "S")
         hm(0, 1, 0)
         hm(0, 1, 1)
-        th(0, 1, 0)
+        inter("s", 0, 0, (0, 2), "G")
         hm(0, 1, 2)
-        inter("s", 0, 0, (1, 2), "V")
         hm(0, 1, 3)
-        inter("s", 0, 0, (0, 1), "S")
-        hm(0, 0, 1)
-        inter("s", 0, 0, (2, 3), "V")
-        hm(0, 0, 2)
-        inter("s", 0, 0, (3, 4), "V")
-        hm(0, 0, 3)
-        th(0, 1, 1)
+        th(0, 0, 1)
         wq("s", 0, 0)
-        th(0, 1, 2)
-        th(0, 1, 3)
-        inter("s", 1, 1, (0, 1), "V")
-        inter("s", 1, 1, (1, 2), "V")
-        inter("s", 1, 1, (3, 4), "S")
-        hm(0, 0, 0)
-        hg(0, 1)
+        th(0, 0, 2)
+        th(0, 0, 3)
+        inter("s", 1, 0, (2, 4), "V")
+        th(0, 1, 0)
         xt(1, 0)
-        th(0, 0, 0)
+        hg(0, 0, "V")
+        inter("s", 0, 1, (2, 4), "S")
         xt(1, 1)
         xc(1, 0, "S")
         xc(1, 1, "S")
-        inter("s", 1, 1, (2, 3), "V")
-        th(0, 0, 1)
-        xq(1)
-        th(0, 0, 2)
-        wq("s", 1, 1)
-        hm(1, 1, 0)
-        th(0, 0, 3)
-        hm(1, 1, 1)
-        inter("m", 0, 0, (1, 2), "V")
-        hm(1, 1, 3)
-        inter("m", 0, 0, (0, 1), "S")
-        inter("m", 0, 0, (2, 3), "V")
-        hm(1, 1, 2)
-        inter("m", 0, 0, (3, 4), "V")
-        hm(1, 0, 1)
-        th(1, 1, 0)
-        hg(0, 0)
-        hm(1, 0, 2)
-        hm(1, 0, 3)
-        inter("s", 1, 0, (1, 2), "S")
-        inter("m", 1, 0, (0, 1), "S")
-        inter("m", 1, 0, (1, 2), "S")
-        inter("s", 1, 0, (0, 1), "V")
-        inter("m", 1, 0, (2, 3), "S")
-        inter("s", 1, 0, (3, 4), "V")
-        hq(0, 1)
-        th(1, 1, 1)
-        inter("p", 0, 0, (1, 2), "V")
-        th(1, 1, 2)
-        inter("p", 0, 0, (3, 4), "V")
+        wq("s", 0, 1)
+        th(0, 1, 1)
         hq(0, 0)
-        th(1, 1, 3)
-        inter("s", 1, 0, (2, 3), "S")
-        wq("m", 0, 0)
+        th(0, 1, 2)
+        xq(1)
+        th(0, 1, 3)
+        inter("s", 1, 0, (0, 2), "G")
+        inter("m", 0, 0, (0, 2), "S")
         hm(1, 0, 0)
-        hg(1, 1)
+        hm(1, 0, 1)
+        hm(1, 0, 2)
+        hg(0, 1, "V")
+        hm(1, 0, 3)
+        hm(1, 1, 0)
         th(1, 0, 0)
-        inter("p", 0, 0, (0, 1), "S")
+        hm(1, 1, 1)
+        hm(1, 1, 2)
+        inter("m", 0, 0, (2, 4), "S")
+        hm(1, 1, 3)
         th(1, 0, 1)
-        th(1, 0, 2)
         wq("s", 1, 0)
+        th(1, 0, 2)
+        hq(0, 1)
         th(1, 0, 3)
-        hq(1, 1)
-        mS(0)
-        inter("p", 0, 0, (2, 3), "S")
-        inter("p", 1, 0, (1, 2), "V")
-        hg(1, 0)
-        inter("p", 1, 0, (0, 1), "S")
-        inter("p", 1, 0, (2, 3), "S")
-        inter("p", 1, 0, (3, 4), "S")
-        e(0)
+        inter("p", 0, 0, (0, 2), "V")
+        th(1, 1, 0)
+        inter("p", 1, 0, (0, 2), "V")
+        inter("p", 0, 0, (2, 4), "S")
+        hg(1, 0, "V")
+        th(1, 1, 1)
+        th(1, 1, 2)
+        th(1, 1, 3)
         wq("p", 0, 0)
-        inter("p", 1, 1, (0, 1), "S")
-        wq("p", 1, 0)
-        mS(1)
-        inter("p", 1, 1, (1, 2), "S")
+        inter("m", 1, 0, (0, 2), "S")
+        mS(0)
         hq(1, 0)
-        mL(0)
+        hg(1, 1, "V")
+        e(0)
+        inter("m", 1, 0, (2, 4), "S")
+        mS(1)
         e(1)
-        inter("m", 1, 1, (2, 3), "V")
-        mL(1)
-        ml(0)
-        inter("p", 1, 1, (3, 4), "S")
-        inter("m", 1, 0, (3, 4), "G")
-        mR(0)
-        ml(1)
-        inter("m", 1, 1, (0, 1), "S")
-        inter("p", 1, 1, (2, 3), "G")
-        ld(0)
-        inter("m", 1, 1, (1, 2), "S")
-        mR(1)
-        ld(1)
-        inter("m", 1, 1, (3, 4), "S")
-        wq("p", 1, 1)
-        mL(2)
-        wq("m", 1, 0)
-        mL(3)
-        ml(2)
-        inter("p", 0, 1, (0, 1), "S")
-        inter("p", 0, 1, (3, 4), "G")
-        mM(0)
-        ml(3)
-        mM(1)
-        inter("p", 0, 1, (1, 2), "S")
-        inter("m", 0, 1, (3, 4), "G")
-        d(0)
+        wq("m", 0, 0)
+        inter("s", 1, 1, (0, 2), "S")
         mS(2)
-        inter("p", 0, 1, (2, 3), "S")
+        wq("m", 1, 0)
+        hq(1, 1)
+        mM(0)
+        e(2)
+        inter("p", 1, 0, (2, 4), "G")
+        mM(1)
+        d(0)
+        inter("s", 1, 1, (2, 4), "S")
+        mS(3)
         d(1)
         mM(2)
-        e(2)
-        z(0, "V")
-        mM(3)
-        inter("m", 0, 1, (0, 1), "S")
-        d(2)
-        mS(3)
-        z(1, "G")
-        d(3)
-        sq(0)
-        mM(4)
-        ld(2)
+        wq("p", 1, 0)
         e(3)
-        mM(5)
-        z(2, "G")
+        mM(3)
+        d(2)
+        z(0, "G")
+        inter("m", 0, 1, (0, 2), "S")
+        mL(0)
+        d(3)
+        mL(1)
+        mS(4)
+        ml(0)
+        inter("m", 0, 1, (2, 4), "S")
+        mR(0)
+        ml(1)
+        z(1, "G")
+        ld(0)
+        e(4)
+        mR(1)
+        ld(1)
+        sq(0)
+        mL(2)
+        pe(0, 0)
+        wq("s", 1, 1)
+        mL(3)
+        mS(5)
         q(0)
         sq(1)
-        mL(4)
-        d(4)
-        inter("m", 0, 1, (1, 2), "S")
-        mS(4)
+        s1(0, 0, "G")
+        mM(4)
         q(1)
-        z(3, "G")
-        mM(6)
-        sq(2)
-        mq(0)
-        mR(2)
-        inter("m", 0, 1, (2, 3), "S")
-        mq(1)
-        qd(0, "G")
-        sq(3)
-        ld(3)
-        mR(3)
-        e(4)
-        q(2)
-        inter("s", 0, 1, (0, 1), "S")
-        wq("m", 0, 1)
-        mL(5)
-        p(0)
-        qd(1, "V")
-        mS(5)
-        d(5)
-        mR(4)
-        z(4, "G")
-        p(1)
-        d(6)
-        q(3)
-        mM(7)
+        mM(5)
+        d(4)
         e(5)
-        s1(0, slice(0, 1), "G")
-        mq(2)
-        ts(0)
-        sq(4)
-        mq(3)
-        s1(1, slice(0, 2), "G")
-        inter("s", 0, 1, (1, 2), "S")
-        q(4)
+        mR(2)
+        s2(0, 0, "G")
+        d(5)
+        inter("m", 1, 1, (0, 2), "S")
+        mqr(0)
+        z(2, "G")
         mS(6)
-        sc(0)
-        ml(4)
-        s2(0, slice(0, 1), "G")
-        mR(5)
+        mR(3)
+        inter("m", 1, 1, (2, 4), "S")
+        q(2)
+        ml(2)
+        mM(6)
         e(6)
-        ml(5)
-        s2(1, slice(0, 2), "G")
-        inter("s", 0, 1, (2, 3), "S")
-        ld(4)
+        qd(0, "G")
+        mM(7)
+        q(3)
+        sq(2)
         mS(7)
-        z(5, "G")
-        inter("s", 0, 1, (3, 4), "S")
-        ld(5)
-        mL(6)
-        mq(4)
+        ld(2)
+        mR(4)
+        mqr(1)
         e(7)
-        mL(7)
-        fd(0, "G")
-        ml(6)
-        sq(5)
-        mR(6)
-        ml(7)
-        qd(4, "G")
-        q(5)
-        ld(6)
-        mR(7)
-        mq(5)
-        wq("s", 0, 1)
-        qd(2, "V")
+        inter("p", 0, 1, (0, 2), "S")
+        mL(4)
+        q(4)
         mS(8)
-        qd(5, "V")
-        p(2)
-        d(7)
-        qd(3, "V")
+        qd(1, "V")
+        mR(5)
+        pe(0, 1)
+        wq("m", 0, 1)
+        mR(6)
         e(8)
-        z(6, "V")
-        p(3)
+        q(5)
+        s1(0, 1, "G")
+        pe(1, 1)
+        d(6)
         mS(9)
-        wq("p", 0, 1)
+        mR(7)
         wq("m", 1, 1)
-        sq(6)
-        mL(8)
-        s1(3, slice(0, 2), "V")
-        p(4)
-        mM(8)
-        q(6)
-        mM(9)
-        s1(2, slice(0, 2), "G")
-        d(8)
-        p(5)
-        mR(8)
-        mq(6)
-        z(7, "G")
-        ld(7)
+        inter("p", 0, 1, (2, 4), "S")
+        d(7)
+        s2(0, 1, "G")
+        tsum(1, 1)
+        ml(3)
         e(9)
-        mM(10)
-        ml(8)
-        mL(9)
-        s2(2, slice(0, 2), "G")
-        d(9)
-        sq(7)
+        z(3, "G")
+        mqr(2)
+        inter("p", 1, 1, (0, 2), "S")
+        ld(3)
+        mM(8)
+        inter("p", 1, 1, (2, 4), "S")
+        qd(2, "G")
+        ml(4)
         mS(10)
-        ld(8)
-        z(8, "G")
-        mM(11)
+        mL(5)
+        d(8)
+        pe(1, 0)
+        mM(9)
+        ld(4)
+        mM(10)
+        d(9)
         e(10)
-        q(7)
-        mL(10)
+        s1(1, 0, "G")
+        mL(6)
         d(10)
-        z(9, "G")
+        sq(3)
         mS(11)
-        sq(8)
-        mq(7)
-        mM(12)
+        ml(5)
+        mM(11)
+        fd(0, "G")
         e(11)
-        ml(9)
-        ts(4)
-        fd(1, "G")
-        q(8)
-        sq(9)
-        ml(10)
+        ml(6)
+        mM(12)
+        pe(2, 1)
+        q(6)
         mS(12)
-        mq(8)
-        z(10, "G")
-        mR(9)
-        e(12)
-        mS(13)
-        s2(3, slice(0, 2), "V")
-        sq(10)
-        qd(6, "V")
-        mR(10)
-        ln(0)
-        qd(7, "V")
-        qd(8, "V")
-        s1(5, slice(0, 2), "V")
+        s2(1, 0, "G")
+        q(7)
+        z(4, "G")
+        cp(1)
+        ld(5)
+        tsum(2, 1)
+        ld(6)
+        pe(2, 0)
         d(11)
-        s1(4, slice(0, 1), "G")
-        d(12)
-        p(6)
+        wq("p", 0, 1)
+        e(12)
+        mL(7)
+        sq(4)
+        wq("p", 1, 1)
+        mS(13)
+        mqr(3)
+        s1(2, 0, "G")
+        mL(8)
+        e(13)
+        mR(8)
+        cp(2)
+        ml(7)
+        z(5, "G")
+        ml(8)
+        mR(9)
+        q(8)
+        mS(14)
+        ld(7)
+        qd(3, "G")
         mM(13)
-        z(11, "G")
+        sq(5)
         q(9)
-        mM(14)
-        d(13)
-        mR(11)
+        mL(9)
+        ld(8)
+        mR(10)
+        pe(3, 0)
+        mqr(4)
+        s2(2, 0, "G")
+        mL(10)
+        e(14)
         q(10)
-        s2(4, slice(0, 1), "G")
-        z(12, "G")
+        qd(4, "G")
+        mR(11)
+        pe(3, 1)
+        d(12)
+        d(13)
+        mS(15)
+        q(11)
+        tsum(3, 1)
+        e(15)
+        s1(3, 0, "G")
+        ml(9)
+        pe(4, 1)
+        mqr(5)
+        z(6, "G")
+        mM(14)
+        cp(3)
         ld(9)
         mM(15)
-        ld(10)
-        p(7)
-        mL(11)
-        mq(9)
-        mL(12)
-        s2(5, slice(0, 2), "V")
-        p(8)
-        ts(6)
-        qd(9, "V")
-        s1(7, slice(0, 2), "V")
-        e(13)
-        s1(8, slice(0, 1), "V")
-        mR(12)
-        s2(7, slice(0, 2), "V")
-        sc(1)
-        s2(8, slice(0, 1), "V")
         d(14)
-        sq(11)
-        s1(6, slice(0, 1), "G")
-        mS(14)
-        ml(11)
-        sq(12)
-        ts(8)
-        z(13, "G")
-        q(11)
-        e(14)
-        q(12)
-        p(9)
-        mS(15)
-        ld(11)
-        s2(6, slice(0, 1), "G")
-        z(14, "G")
-        mR(13)
-        ml(12)
-        sq(13)
-        mq(10)
-        e(15)
-        mL(13)
-        ld(12)
-        qd(10, "G")
-        sq(14)
-        mR(14)
-        q(13)
-        ln(1)
-        ml(13)
-        s1(9, slice(0, 1), "G")
-        mL(14)
+        pe(4, 0)
+        mL(11)
         d(15)
+        mR(12)
+        qd(5, "G")
+        sq(6)
+        ml(10)
+        ml(11)
+        mR(13)
+        q(12)
+        q(13)
+        s2(3, 0, "G")
+        mR(14)
+        pe(5, 1)
+        ld(10)
+        z(7, "G")
         mR(15)
+        ld(11)
+        mqr(6)
+        pe(5, 0)
+        mL(12)
+        mL(13)
+        s1(4, 0, "G")
+        ml(12)
+        sq(7)
+        tsum(5, 0)
+        ml(13)
+        qd(6, "G")
+        ld(12)
         q(14)
-        s2(9, slice(0, 1), "G")
-        ld(13)
-        z(15, "G")
-        ts(9)
-        ml(14)
-        p(10)
-        mq(11)
-        t1(1, "G")
-        mL(15)
-        mq(12)
-        ld(14)
-        fd(2, "G")
-        mq(13)
-        mq(14)
-        sq(15)
-        ts(10)
-        s1(10, slice(0, 1), "G")
-        ml(15)
         q(15)
-        s2(10, slice(0, 1), "G")
+        mL(14)
+        tsum(5, 1)
+        ld(13)
+        s2(4, 0, "G")
+        pe(6, 1)
+        mqr(7)
+        s1(4, 1, "G")
+        pe(6, 0)
+        ml(14)
+        mL(15)
+        qd(7, "G")
+        cp(5)
+        ld(14)
+        ml(15)
+        tsum(6, 0)
         ld(15)
-        sc(2)
-        qd(11, "V")
-        qd(12, "V")
-        p(11)
-        qd(13, "V")
-        qd(14, "V")
-        p(12)
-        s1(11, slice(0, 2), "V")
-        mq(15)
-        p(13)
-        ts(12)
-        s2(11, slice(0, 2), "V")
-        qd(15, "V")
-        p(14)
-        s1(12, slice(0, 1), "V")
-        s1(13, slice(0, 1), "V")
-        ts(13)
-        s2(12, slice(0, 1), "V")
-        s2(13, slice(0, 1), "V")
+        s2(4, 1, "G")
+        pe(7, 1)
+        fd(1, "V")
+        tsum(6, 1)
+        pe(7, 0)
+        fd(2, "V")
+        fd(3, "V")
+        ln(0)
+        s1(7, 0, "V")
+        s2(7, 0, "V")
+        s1(7, 1, "V")
+        s2(7, 1, "V")
+        ln(1)
         t1(0, "V")
-        p(15)
-        s1(14, slice(0, 1), "V")
-        ts(14)
         o(0)
+        cp(6)
+        t1(1, "V")
         ln(2)
-        s2(14, slice(0, 1), "V")
-        s1(15, slice(0, 1), "V")
         ob(0, "V")
-        ts(15)
-        s2(15, slice(0, 1), "V")
-        oq(0)
         o(1)
-        fd(3, "G")
-        ob(1, "S")
-        sc(3)
-        oq(1)
-        t1(2, "V")
         la(3)
-        o(2)
-        ln(3)
+        oq(0)
+        t1(2, "V")
+        ob(1, "S")
         t1(3, "V")
-        ob(2, "S")
+        ln(3)
+        oq(1)
+        o(2)
         oa(3)
-        oq(2)
+        ob(2, "S")
         o(3)
+        oq(2)
         ob(3, "V")
         oq(3)

@@ -413,328 +413,330 @@ def tile_mixturedensitynetworkelementwisenll_x2_kernel(
         hm(0, 0, 1)
         th(0, 0, 0)
         hm(0, 0, 2)
-        inter("s", 0, 1, (0, 2), "V")
         hm(0, 0, 3)
+        inter("s", 0, 0, (0, 2), "G")
         inter("s", 0, 0, (2, 4), "S")
         hm(0, 1, 0)
         hm(0, 1, 1)
-        inter("s", 0, 0, (0, 2), "G")
         hm(0, 1, 2)
         hm(0, 1, 3)
+        inter("s", 0, 1, (0, 2), "G")
         th(0, 0, 1)
-        wq("s", 0, 0)
         th(0, 0, 2)
         th(0, 0, 3)
         inter("s", 1, 0, (2, 4), "V")
         th(0, 1, 0)
+        wq("s", 0, 0)
         xt(1, 0)
-        hg(0, 0, "V")
         inter("s", 0, 1, (2, 4), "S")
+        hg(0, 0, "V")
         xt(1, 1)
         xc(1, 0, "S")
         xc(1, 1, "S")
-        wq("s", 0, 1)
         th(0, 1, 1)
-        hq(0, 0)
-        th(0, 1, 2)
         xq(1)
+        th(0, 1, 2)
+        hq(0, 0)
         th(0, 1, 3)
-        inter("s", 1, 0, (0, 2), "G")
+        wq("s", 0, 1)
         inter("m", 0, 0, (0, 2), "S")
         hm(1, 0, 0)
         hm(1, 0, 1)
-        hm(1, 0, 2)
         hg(0, 1, "V")
+        hm(1, 0, 2)
         hm(1, 0, 3)
-        hm(1, 1, 0)
         th(1, 0, 0)
+        hm(1, 1, 0)
         hm(1, 1, 1)
-        hm(1, 1, 2)
         inter("m", 0, 0, (2, 4), "S")
+        hm(1, 1, 2)
         hm(1, 1, 3)
+        inter("s", 1, 0, (0, 2), "G")
         th(1, 0, 1)
-        wq("s", 1, 0)
         th(1, 0, 2)
         hq(0, 1)
         th(1, 0, 3)
-        inter("p", 0, 0, (0, 2), "V")
         th(1, 1, 0)
-        inter("p", 1, 0, (0, 2), "V")
+        wq("s", 1, 0)
         inter("p", 0, 0, (2, 4), "S")
-        hg(1, 0, "V")
+        inter("p", 0, 0, (0, 2), "V")
+        wq("m", 0, 0)
         th(1, 1, 1)
-        th(1, 1, 2)
-        th(1, 1, 3)
         wq("p", 0, 0)
-        inter("m", 1, 0, (0, 2), "S")
+        th(1, 1, 2)
+        hg(1, 0, "V")
+        th(1, 1, 3)
+        inter("p", 1, 0, (0, 2), "S")
         mS(0)
-        hq(1, 0)
+        inter("p", 1, 0, (2, 4), "S")
         hg(1, 1, "V")
         e(0)
-        inter("m", 1, 0, (2, 4), "S")
+        inter("m", 1, 0, (0, 2), "S")
         mS(1)
+        hq(1, 0)
         e(1)
-        wq("m", 0, 0)
-        inter("s", 1, 1, (0, 2), "S")
+        wq("p", 1, 0)
+        inter("m", 1, 0, (2, 4), "S")
         mS(2)
-        wq("m", 1, 0)
         hq(1, 1)
-        mM(0)
+        mL(0)
         e(2)
-        inter("p", 1, 0, (2, 4), "G")
-        mM(1)
-        d(0)
-        inter("s", 1, 1, (2, 4), "S")
+        mL(1)
+        wq("m", 1, 0)
+        inter("s", 1, 1, (0, 2), "S")
         mS(3)
+        ml(0)
+        mM(0)
+        ml(1)
+        e(3)
+        mM(1)
+        ld(0)
+        inter("s", 1, 1, (2, 4), "S")
+        mS(4)
+        ld(1)
+        mL(2)
+        d(0)
+        pe(0, 0)
+        mL(3)
         d(1)
         mM(2)
-        wq("p", 1, 0)
-        e(3)
-        mM(3)
-        d(2)
-        z(0, "G")
-        inter("m", 0, 1, (0, 2), "S")
-        mL(0)
-        d(3)
-        mL(1)
-        mS(4)
-        ml(0)
-        inter("m", 0, 1, (2, 4), "S")
-        mR(0)
-        ml(1)
-        z(1, "G")
-        ld(0)
-        e(4)
-        mR(1)
-        ld(1)
-        sq(0)
-        mL(2)
-        pe(0, 0)
         wq("s", 1, 1)
-        mL(3)
-        mS(5)
-        q(0)
-        sq(1)
+        inter("m", 0, 1, (0, 2), "S")
+        mM(3)
         s1(0, 0, "G")
-        mM(4)
-        q(1)
-        mM(5)
-        d(4)
-        e(5)
-        mR(2)
-        s2(0, 0, "G")
-        d(5)
+        d(2)
+        mR(0)
+        d(3)
+        inter("m", 0, 1, (2, 4), "S")
+        ml(2)
+        z(0, "G")
+        mR(1)
+        ml(3)
         inter("m", 1, 1, (0, 2), "S")
+        ld(2)
+        mM(4)
+        ld(3)
+        inter("m", 1, 1, (2, 4), "S")
+        mL(4)
+        d(4)
+        z(1, "G")
+        mL(5)
+        ml(4)
+        mM(5)
+        pe(1, 0)
+        ml(5)
+        mM(6)
+        ld(4)
+        e(4)
+        sq(0)
+        ld(5)
+        s2(0, 0, "G")
+        mL(6)
+        d(5)
+        mL(7)
+        s1(1, 0, "G")
+        pe(2, 0)
+        q(0)
+        mS(5)
+        q(1)
+        mM(7)
+        e(5)
+        wq("m", 0, 1)
+        mR(2)
+        sq(1)
+        wq("m", 1, 1)
+        mS(6)
         mqr(0)
         z(2, "G")
-        mS(6)
+        inter("p", 0, 1, (0, 2), "S")
         mR(3)
-        inter("m", 1, 1, (2, 4), "S")
         q(2)
-        ml(2)
-        mM(6)
         e(6)
-        qd(0, "G")
-        mM(7)
         q(3)
+        inter("p", 0, 1, (2, 4), "S")
+        mR(4)
+        ml(6)
+        qd(0, "G")
+        mqr(1)
         sq(2)
         mS(7)
-        ld(2)
-        mR(4)
-        mqr(1)
+        mR(5)
         e(7)
-        inter("p", 0, 1, (0, 2), "S")
-        mL(4)
+        ml(7)
+        inter("p", 1, 1, (0, 2), "S")
         q(4)
         mS(8)
-        qd(1, "V")
-        mR(5)
-        pe(0, 1)
-        wq("m", 0, 1)
-        mR(6)
-        e(8)
-        q(5)
-        s1(0, 1, "G")
-        pe(1, 1)
-        d(6)
-        mS(9)
-        mR(7)
-        wq("m", 1, 1)
-        inter("p", 0, 1, (2, 4), "S")
-        d(7)
-        s2(0, 1, "G")
-        tsum(1, 1)
-        ml(3)
-        e(9)
-        z(3, "G")
-        mqr(2)
-        inter("p", 1, 1, (0, 2), "S")
-        ld(3)
-        mM(8)
-        inter("p", 1, 1, (2, 4), "S")
-        qd(2, "G")
-        ml(4)
-        mS(10)
-        mL(5)
-        d(8)
-        pe(1, 0)
-        mM(9)
-        ld(4)
-        mM(10)
-        d(9)
-        e(10)
-        s1(1, 0, "G")
-        mL(6)
-        d(10)
-        sq(3)
-        mS(11)
-        ml(5)
-        mM(11)
         fd(0, "G")
-        e(11)
-        ml(6)
-        mM(12)
-        pe(2, 1)
-        q(6)
-        mS(12)
+        q(5)
+        mR(6)
+        pe(0, 1)
+        d(6)
         s2(1, 0, "G")
-        q(7)
-        z(4, "G")
-        cp(1)
-        ld(5)
-        tsum(2, 1)
-        ld(6)
-        pe(2, 0)
-        d(11)
-        wq("p", 0, 1)
-        e(12)
-        mL(7)
-        sq(4)
-        wq("p", 1, 1)
-        mS(13)
-        mqr(3)
+        d(7)
+        mM(8)
+        e(8)
         s1(2, 0, "G")
-        mL(8)
-        e(13)
+        mqr(2)
+        mM(9)
+        inter("p", 1, 1, (2, 4), "S")
+        mS(9)
+        qd(1, "V")
+        mR(7)
+        e(9)
+        wq("p", 0, 1)
+        mS(10)
+        pe(1, 1)
+        qd(2, "G")
+        d(8)
+        d(9)
+        tsum(1, 1)
+        wq("p", 1, 1)
+        pe(2, 1)
+        z(3, "V")
+        mM(10)
+        cp(1)
+        mM(11)
+        z(4, "G")
+        d(10)
+        e(10)
+        tsum(2, 1)
+        d(11)
+        sq(3)
+        q(6)
+        s2(2, 0, "G")
+        q(7)
+        sq(4)
+        mS(11)
+        s1(0, 1, "V")
         mR(8)
         cp(2)
-        ml(7)
+        mqr(3)
+        e(11)
         z(5, "G")
-        ml(8)
+        mS(12)
+        ld(6)
         mR(9)
-        q(8)
-        mS(14)
+        e(12)
         ld(7)
-        qd(3, "G")
-        mM(13)
-        sq(5)
+        q(8)
+        pe(3, 0)
+        mL(8)
         q(9)
         mL(9)
-        ld(8)
-        mR(10)
-        pe(3, 0)
+        qd(3, "G")
+        ml(8)
+        sq(5)
+        mS(13)
         mqr(4)
-        s2(2, 0, "G")
-        mL(10)
-        e(14)
-        q(10)
-        qd(4, "G")
-        mR(11)
+        mM(12)
+        e(13)
+        mM(13)
+        ld(8)
+        mS(14)
         pe(3, 1)
+        s2(0, 1, "V")
+        mR(10)
+        qd(4, "V")
+        e(14)
+        mL(10)
+        s1(3, 0, "G")
+        q(10)
+        pe(4, 1)
+        tsum(3, 1)
         d(12)
         d(13)
-        mS(15)
-        q(11)
-        tsum(3, 1)
-        e(15)
-        s1(3, 0, "G")
+        s2(3, 0, "G")
         ml(9)
-        pe(4, 1)
-        mqr(5)
         z(6, "G")
-        mM(14)
-        cp(3)
-        ld(9)
-        mM(15)
-        d(14)
-        pe(4, 0)
-        mL(11)
-        d(15)
-        mR(12)
-        qd(5, "G")
-        sq(6)
         ml(10)
+        mS(15)
+        ld(9)
+        cp(3)
+        mR(11)
+        ld(10)
+        pe(4, 0)
+        fd(1, "V")
+        mL(11)
+        e(15)
+        s1(4, 0, "G")
+        q(11)
+        mL(12)
+        sq(6)
+        mM(14)
         ml(11)
+        mM(15)
+        mqr(5)
+        s2(4, 0, "G")
+        mR(12)
+        ld(11)
+        qd(5, "G")
         mR(13)
         q(12)
-        q(13)
-        s2(3, 0, "G")
-        mR(14)
-        pe(5, 1)
-        ld(10)
-        z(7, "G")
-        mR(15)
-        ld(11)
-        mqr(6)
         pe(5, 0)
-        mL(12)
+        d(14)
         mL(13)
-        s1(4, 0, "G")
-        ml(12)
-        sq(7)
+        q(13)
         tsum(5, 0)
+        d(15)
+        fd(2, "G")
+        pe(5, 1)
+        ml(12)
         ml(13)
-        qd(6, "G")
+        z(7, "G")
         ld(12)
-        q(14)
-        q(15)
-        mL(14)
-        tsum(5, 1)
         ld(13)
-        s2(4, 0, "G")
-        pe(6, 1)
-        mqr(7)
-        s1(4, 1, "G")
+        tsum(5, 1)
         pe(6, 0)
-        ml(14)
-        mL(15)
-        qd(7, "G")
+        s1(4, 1, "V")
+        sq(7)
+        mqa(6)
+        s2(4, 1, "V")
+        mL(14)
         cp(5)
-        ld(14)
-        ml(15)
-        tsum(6, 0)
-        ld(15)
-        s2(4, 1, "G")
-        pe(7, 1)
-        fd(1, "V")
-        tsum(6, 1)
-        pe(7, 0)
-        fd(2, "V")
-        fd(3, "V")
+        mqb(6)
+        mL(15)
+        s1(6, 0, "G")
+        ml(14)
         ln(0)
-        s1(7, 0, "V")
-        s2(7, 0, "V")
-        s1(7, 1, "V")
-        s2(7, 1, "V")
+        mR(14)
+        ml(15)
+        qd(6, "G")
+        ld(14)
+        mR(15)
+        q(14)
+        ld(15)
         ln(1)
+        q(15)
         t1(0, "V")
+        pe(7, 0)
+        s2(6, 0, "G")
+        mqr(7)
         o(0)
-        cp(6)
-        t1(1, "V")
-        ln(2)
+        qd(7, "V")
+        pe(6, 1)
+        s1(7, 0, "V")
         ob(0, "V")
-        o(1)
-        la(3)
+        pe(7, 1)
+        tsum(6, 1)
+        t1(1, "V")
         oq(0)
-        t1(2, "V")
-        ob(1, "S")
-        t1(3, "V")
-        ln(3)
+        o(1)
+        ln(2)
+        fd(3, "V")
+        ob(1, "V")
+        s2(7, 0, "V")
         oq(1)
+        s1(7, 1, "V")
+        cp(6)
+        t1(2, "V")
+        la(3)
+        s2(7, 1, "V")
         o(2)
-        oa(3)
+        ln(3)
+        t1(3, "V")
         ob(2, "S")
-        o(3)
+        oa(3)
         oq(2)
+        o(3)
         ob(3, "V")
         oq(3)

from contextlib import ExitStack
import math

import concourse.mybir as mybir
from concourse.masks import make_identity

F32 = mybir.dt.float32
BF16 = mybir.dt.bfloat16
U32 = mybir.dt.uint32
I32 = mybir.dt.int32
U8 = mybir.dt.uint8
FP8X4 = mybir.dt.float8_e4m3fn_x4
ACT = mybir.ActivationFunctionType
ALU = mybir.AluOpType
AX = mybir.AxisListType

N, D, F, K, T = 1024, 512, 1024, 4, 256
FLOPS = 2 * N * D * F + 2 * N * F * 3 * K * T
HALF_LOG_2PI = 0.5 * math.log(2.0 * math.pi)
ROOT_HALF = math.sqrt(0.5)
P = 128
PS = {"S": 1, "M": 2, "L": 2, "R": 2, "sum": 1}
HTAG = "SMRLMRLS"


def tile_mixturedensitynetworkelementwisenll_x2_kernel(
    tc, x, y, w1_words, w1_scales, gain, wp, wm, ws, out_0, out_1, out_2
):
    nc = tc.nc
    with ExitStack() as ctx:
        keep = ctx.enter_context(tc.tile_pool(name="keep", bufs=1))
        work = ctx.enter_context(tc.tile_pool(name="work", bufs=3))
        psum = ctx.enter_context(tc.psum_pool(name="psum", bufs=1))
        ctx.enter_context(tc.manual_schedule())
        ENG = {"V": nc.vector, "G": nc.gpsimd}

        def bank(name, shape, tag):
            return psum.tile(shape, F32, name=name, tag=tag, bufs=PS[tag])

        dummy = keep.tile([P, 1], F32, name="dummy")
        nc.vector.memset(dummy[:], 0.0)
        nc.scalar.activation(out=dummy[:], in_=dummy[:], func=ACT.Exp)
        ident = keep.tile([P, P], F32, name="ident")
        make_identity(nc, ident[:])
        w1s_raw = keep.tile([P, F], U8, name="w1s_raw", align_bytes=64)
        nc.vector.memset(w1s_raw[:].bitcast(I32), 0)
        for q in range(4):
            nc.scalar.dma_start(
                out=w1s_raw[32 * q : 32 * q + 4, :].bitcast(I32),
                in_=w1_scales[0][4 * q : 4 * q + 4, :].bitcast(I32),
            )
        gain_sb = keep.tile([P, 2, 4], BF16, name="gain_sb")
        nc.scalar.dma_start(out=gain_sb[:], in_=gain.rearrange("(f p t) -> p f t", f=2, t=4))

        def ring(shape, dtype, name):
            return work.tile(shape, dtype, name=name, tag="wi", align_bytes=64, bufs=8)

        x_sb0 = ring([P, 4, D], BF16, "x_sb0")
        w1_raw = ring([P, F], U32, "w1_raw")
        x_sb1 = ring([P, 4, D], BF16, "x_sb1")
        x_sb = [x_sb0, x_sb1]
        y_sb = keep.tile([P, 2, 4, T], BF16, name="y_sb")
        w_hbm = {"s": ws, "m": wm, "p": wp}
        w_raw = {(w, f): keep.tile([P, 4, K * T], BF16, name="w_raw_%s%d" % (w, f)) for w in "smp" for f in range(2)}

        def load_x(g, a, b):
            src = x[512 * g : 512 * g + 512, :].rearrange("(p j) d -> p j d", j=4)
            nc.sync.dma_start(out=x_sb[g][:, a:b, :], in_=src[:, a:b, :])

        def load_w(w, f):
            src = w_hbm[w][512 * f : 512 * f + 512].rearrange("(p j) k t -> p j (k t)", j=4)
            nc.sync.dma_start(out=w_raw[w, f][:], in_=src)

        load_x(0, 0, 2)
        load_x(0, 2, 4)
        nc.sync.dma_start(out=w1_raw[:].bitcast(I32), in_=w1_words[0].rearrange("p n t -> p (n t)").bitcast(I32))
        load_w("s", 0)
        load_w("s", 1)
        load_x(1, 0, 4)
        nc.sync.dma_start(out=y_sb[:], in_=y.rearrange("(g p j) t -> p g j t", g=2, j=4))
        load_w("m", 0)
        load_w("m", 1)
        load_w("p", 0)
        load_w("p", 1)

        def codes(name, n):
            return keep.tile([P, n], U32, name=name + "c", align_bytes=64), keep.tile([P, n], U8, name=name + "s", align_bytes=64)

        x_q = [codes("xq%d" % g, 512) for g in range(2)]
        w1_q = codes("w1q", F)
        h_q = {(g, f): codes("hq%d%d" % (g, f), 512) for g in range(2) for f in range(2)}
        w_q = {(w, f, h): codes("wq%s%d%d" % (w, f, h), 512) for w in "smp" for f in range(2) for h in range(2)}

        xts = {}
        xgs = {}

        def xt(g, b):
            words = x_sb[g][:].rearrange("p j d -> p (j d)").bitcast(F32)
            t = bank("xt", [P, 2, 2, P], "LR"[b])
            xts[g, b] = t
            for jj in range(2):
                for u in range(2):
                    j = 2 * b + jj
                    nc.tensor.transpose(t[:, jj, u, :], words[:, 256 * j + u : 256 * (j + 1) : 2], ident[:])

        def xc(g, b, eng):
            if g not in xgs:
                xgs[g] = ring([P, 2048], BF16, "xg")
            dst = xgs[g][:].bitcast(F32).rearrange("p (j r u) -> p j r u", j=4, u=2)[:, 2 * b : 2 * b + 2]
            src = xts[g, b][:].rearrange("p j u r -> p j r u")
            if eng == "S":
                nc.scalar.copy(dst, src)
            else:
                nc.vector.tensor_copy(out=dst, in_=src)

        def quant(q, cols, src):
            nc.vector.quantize_mx(out=q[0][:, cols].bitcast(FP8X4), scales=q[1][:, cols], in_=src)

        ALL = slice(0, 512)

        def xq(g):
            quant(x_q[g], ALL, xgs[g][:])

        def w1s():
            nc.vector.tensor_copy(
                out=w1_q[1][:].rearrange("p (f t m) -> p f m t", f=2, t=4),
                in_=w1s_raw[:].rearrange("p (f m t) -> p f m t", f=2, t=4),
            )

        def w1c():
            nc.vector.tensor_copy(
                out=w1_q[0][:].bitcast(I32).rearrange("p (f t m) -> p f t m", f=2, t=4),
                in_=w1_raw[:].bitcast(I32).rearrange("p (f m t) -> p f t m", f=2, t=4),
            )

        def mx(out, a, acols, b, bcols, start, stop):
            nc.tensor.matmul_mx(
                out=out,
                lhsT=a[0][:, acols].bitcast(FP8X4),
                lhsT_scale=a[1][:, acols],
                rhs=b[0][:, bcols].bitcast(FP8X4),
                rhs_scale=b[1][:, bcols],
                start=start,
                stop=stop,
            )

        acc1 = {}
        ths = {}
        hb = {}

        def hm(g, f, t):
            acc1[g, f, t] = bank("acc1", [P, 512], HTAG[4 * f + t])
            c = 4 * f + t
            mx(acc1[g, f, t][:], w1_q, slice(c * P, c * P + P), x_q[g], ALL, True, True)

        def th(g, f, t):
            if (g, f) not in ths:
                ths[g, f] = work.tile([P, 4, 512], F32, name="ths", bufs=2)
            nc.scalar.activation(out=ths[g, f][:, t, :], in_=acc1[g, f, t][:], func=ACT.Tanh)

        def hg(g, f, eng="V"):
            h = ring([P, 512, 4], BF16, "h")
            ENG[eng].tensor_tensor(
                out=h[:].rearrange("p (c i) t -> p c t i", i=4),
                in0=ths[g, f][:].rearrange("p t (c i) -> p c t i", i=4),
                in1=gain_sb[:, f, :].unsqueeze(1).unsqueeze(3).to_broadcast([P, 128, 4, 4]),
                op=ALU.mult,
            )
            hb[g, f] = h

        def hq(g, f):
            quant(h_q[g, f], ALL, hb[g, f][:].rearrange("p n t -> p (n t)"))

        wi = {}

        def inter(w, f, h, k, eng):
            if (w, f, h) not in wi:
                wi[w, f, h] = ring([P, 512, 4], BF16, "wi")
            ks = k if w is None else slice(k[0], k[1])
            src = w_raw[w, f][:].rearrange("p j (k h t) -> p h k t j", k=4, h=2)[:, h, ks]
            dst = wi[w, f, h][:].rearrange("p (k t) j -> p k t j", k=4)[:, ks]
            sign = -1.0 if w == "s" else 1.0
            if eng == "S" and w == "s":
                nc.scalar.activation(out=dst, in_=src, func=ACT.Copy, scale=sign)
            elif eng == "S":
                nc.scalar.copy(dst, src)
            elif eng == "V":
                nc.vector.tensor_scalar(out=dst, in0=src, scalar1=sign, scalar2=None, op0=ALU.mult)
            else:
                nc.gpsimd.tensor_scalar(out=dst, in0=src, scalar1=sign, scalar2=0.0, op0=ALU.mult, op1=ALU.add)

        def wq(w, f, h):
            quant(w_q[w, f, h], ALL, wi[w, f, h][:].rearrange("p c j -> p (c j)"))

        units = [(h, g, j) for h in range(2) for g in range(2) for j in range(4)]
        ab = [keep.tile([P, 2, 4, P], F32, name="ab%d" % b) for b in range(4)]
        mxs = [keep.tile([P, 2, 4, P], F32, name="mx%d" % b) for b in range(4)]
        osp = [keep.tile([P, T], U8, name="os%d" % g, align_bytes=64) for g in range(2)]
        acc = {}
        dt = {}
        et = {}
        xx = {}
        sb = {}
        SUMJ = {}
        ot = {}

        def mm(u, tag, names):
            h, g, j = units[u]
            a = bank("acc" + tag, [P, 4, P], tag)
            acc[u, tag] = a
            passes = [(w, f) for w in names for f in range(2)]
            for i, (w, f) in enumerate(passes):
                mx(
                    a[:].rearrange("p k t -> p (k t)"),
                    h_q[g, f],
                    slice(j * P, j * P + P),
                    w_q[w, f, h],
                    ALL,
                    i == 0,
                    i == len(passes) - 1,
                )

        def mS(u):
            mm(u, "S", "s")

        def mM(u):
            mm(u, "M", "m")

        def mL(u):
            mm(u, "L", "p")

        def mR(u):
            mm(u, "R", "ps")

        def wide(ap):
            return ap.unsqueeze(1).to_broadcast([P, 4, P])

        def get(d, k, shape, name, bufs, tag=None):
            if k not in d:
                t = work.tile(shape, F32, name=name, tag=tag or name, bufs=bufs)
                d[k] = t
            return d[k]

        def e(u):
            t = get(et, u // 2, [P, 2, 4, P], "et", 2)
            nc.scalar.activation(out=t[:, u % 2], in_=acc[u, "S"][:], func=ACT.Exp)

        def d(u):
            h, g, j = units[u]
            t = get(dt, u // 2, [P, 2, 4, P], "dt", 3)
            nc.vector.tensor_tensor(
                out=t[:, u % 2], in0=acc[u, "M"][:], in1=wide(y_sb[:, g, j, h * P : h * P + P]), op=ALU.subtract
            )

        def z(v, eng):
            ENG[eng].tensor_tensor(out=dt[v][:], in0=dt[v][:], in1=et[v][:], op=ALU.mult)

        def sq(v):
            nc.scalar.activation(out=dt[v][:], in_=dt[v][:], func=ACT.Square, scale=ROOT_HALF)

        def ml(u):
            nc.vector.tensor_reduce(
                out=mxs[u // 4][:, 0, u % 4, :], in_=acc[u, "L"][:].rearrange("p k t -> p t k"), axis=AX.X, op=ALU.max
            )

        def ld(u):
            t = get(xx, u // 2, [P, 2, 2, 4, P], "xx", 3)
            nc.vector.tensor_tensor(
                out=t[:, 0, u % 2], in0=acc[u, "L"][:], in1=wide(mxs[u // 4][:, 0, u % 4, :]), op=ALU.subtract
            )

        def q(u):
            nc.vector.tensor_tensor(
                out=dt[u // 2][:, u % 2], in0=acc[u, "R"][:], in1=dt[u // 2][:, u % 2], op=ALU.subtract
            )

        m1 = {}

        def pair(v):
            return v // 2, slice(2 * (v % 2), 2 * (v % 2) + 2)

        def mqa(v):
            t = get(m1, v, [P, 2, 2, P], "m1", 1)
            nc.vector.tensor_tensor(out=t[:], in0=dt[v][:, :, 0:2], in1=dt[v][:, :, 2:4], op=ALU.max)

        def mqr(v):
            b, js = pair(v)
            nc.vector.tensor_reduce(
                out=mxs[b][:, 1, js, :], in_=dt[v][:].rearrange("p a k t -> p a t k"), axis=AX.X, op=ALU.max
            )

        def mqb(v):
            b, js = pair(v)
            nc.vector.tensor_tensor(out=mxs[b][:, 1, js, :], in0=m1[v][:, :, 0], in1=m1[v][:, :, 1], op=ALU.max)

        def qd(v, eng):
            b, js = pair(v)
            t = get(xx, v, [P, 2, 2, 4, P], "xx", 3)
            ENG[eng].tensor_tensor(
                out=t[:, 1],
                in0=dt[v][:],
                in1=mxs[b][:, 1, js, :].unsqueeze(2).to_broadcast([P, 2, 4, P]),
                op=ALU.subtract,
            )

        def pe(v, a):
            nc.scalar.activation(out=xx[v][:, a], in_=xx[v][:, a], func=ACT.Exp)

        def tsum(v, a):
            t = sb.get(v)
            if t is None:
                t = bank("sb", [P, 2, 2, P], "sum")
                sb[v] = t
                SUMJ[v] = []
            SUMJ[v].append(a)
            for k in range(4):
                nc.tensor.matmul(out=t[:, a], lhsT=ident[:], rhs=xx[v][:, a, :, k, :], start=(k == 0), stop=(k == 3))

        def cp(v):
            b, js = pair(v)
            if len(SUMJ[v]) == 2:
                nc.scalar.copy(ab[b][:, :, js, :], sb[v][:])
            else:
                a = SUMJ[v][0]
                nc.scalar.copy(ab[b][:, a, js, :], sb[v][:, a])

        st1 = {}

        def s1(v, a, eng):
            t = get(st1, (v, a), [P, 2, 2, P], "s1", 1)
            ENG[eng].tensor_tensor(out=t[:], in0=xx[v][:, a, :, 0:2], in1=xx[v][:, a, :, 2:4], op=ALU.add)

        def s2(v, a, eng):
            b, js = pair(v)
            t = st1[v, a]
            ENG[eng].tensor_tensor(out=ab[b][:, a, js, :], in0=t[:, :, 0], in1=t[:, :, 1], op=ALU.add)

        def fd(b, eng="G"):
            ENG[eng].tensor_tensor(out=mxs[b][:, 0], in0=mxs[b][:, 0], in1=mxs[b][:, 1], op=ALU.subtract)

        def flat(t):
            return t[:].rearrange("p a j t -> p (a j t)")

        def la(b):
            nc.scalar.activation(out=flat(ab[b])[:, 0:768], in_=flat(ab[b])[:, 0:768], func=ACT.Ln)

        def ln(b):
            c = 768 if b == 3 else 0
            nc.scalar.activation(out=flat(ab[b])[:, c:1024], in_=flat(ab[b])[:, c:1024], func=ACT.Ln)

        def t1(b, eng="G"):
            ENG[eng].tensor_tensor(out=mxs[b][:, 0], in0=mxs[b][:, 0], in1=ab[b][:, 0], op=ALU.add)

        def opart(b, js):
            if b not in ot:
                ot[b] = work.tile([P, 4, P], F32, name="o", bufs=2)
            nc.vector.scalar_tensor_tensor(
                out=ot[b][:, js],
                in0=mxs[b][:, 0, js],
                scalar=HALF_LOG_2PI,
                in1=ab[b][:, 1, js],
                op0=ALU.add,
                op1=ALU.subtract,
            )

        def oa(b):
            opart(b, slice(0, 2))

        def o(b):
            h, g = b // 2, b % 2
            opart(b, slice(2, 4) if b == 3 else slice(0, 4))
            v = ot[b]
            nc.sync.dma_start(
                out=out_0[512 * g : 512 * g + 512, h * P : h * P + P].rearrange("(p j) t -> p j t", j=4), in_=v[:]
            )

        obt = {}

        def ob(b, eng):
            obt[b] = work.tile([P, P, 4], BF16, name="ob", bufs=1, align_bytes=64)
            src = ot[b][:].rearrange("p j (c i) -> p c j i", i=4)
            dst = obt[b][:].rearrange("p (c i) j -> p c j i", i=4)
            if eng == "S":
                nc.scalar.copy(dst, src)
            else:
                nc.vector.tensor_copy(out=dst, in_=src)

        def oq(b):
            h, g = b // 2, b % 2
            cols = slice(h * P, h * P + P)
            oc = work.tile([P, P], U32, name="oc", bufs=1, align_bytes=64)
            nc.vector.quantize_mx(
                out=oc[:].bitcast(FP8X4), scales=osp[g][:, cols], in_=obt[b][:].rearrange("p t j -> p (t j)")
            )
            nc.sync.dma_start(
                out=out_1[g][:, cols, :].rearrange("p m b -> p (m b)").bitcast(I32), in_=oc[:].bitcast(I32)
            )
            if h == 1:
                for qq in range(4):
                    nc.sync.dma_start(
                        out=out_2[g][4 * qq : 4 * qq + 4, :].bitcast(I32),
                        in_=osp[g][32 * qq : 32 * qq + 4, :].bitcast(I32),
                    )

        w1s()
        xt(0, 0)
        xt(0, 1)
        xc(0, 0, "S")
        xc(0, 1, "S")
        w1c()
        xq(0)
        hm(0, 0, 0)
        hm(0, 0, 1)
        th(0, 0, 0)
        hm(0, 0, 2)
        hm(0, 0, 3)
        inter("s", 0, 0, (0, 2), "G")
        inter("s", 0, 0, (2, 4), "S")
        hm(0, 1, 0)
        hm(0, 1, 1)
        hm(0, 1, 2)
        hm(0, 1, 3)
        inter("s", 0, 1, (0, 2), "G")
        th(0, 0, 1)
        th(0, 0, 2)
        th(0, 0, 3)
        inter("s", 1, 0, (2, 4), "V")
        th(0, 1, 0)
        wq("s", 0, 0)
        xt(1, 0)
        inter("s", 0, 1, (2, 4), "S")
        hg(0, 0, "V")
        xt(1, 1)
        xc(1, 0, "S")
        xc(1, 1, "S")
        th(0, 1, 1)
        xq(1)
        th(0, 1, 2)
        hq(0, 0)
        th(0, 1, 3)
        wq("s", 0, 1)
        inter("m", 0, 0, (0, 2), "S")
        hm(1, 0, 0)
        hm(1, 0, 1)
        hg(0, 1, "V")
        hm(1, 0, 2)
        hm(1, 0, 3)
        th(1, 0, 0)
        hm(1, 1, 0)
        hm(1, 1, 1)
        inter("m", 0, 0, (2, 4), "S")
        hm(1, 1, 2)
        hm(1, 1, 3)
        inter("s", 1, 0, (0, 2), "G")
        th(1, 0, 1)
        th(1, 0, 2)
        hq(0, 1)
        th(1, 0, 3)
        th(1, 1, 0)
        wq("s", 1, 0)
        inter("p", 0, 0, (2, 4), "S")
        inter("p", 0, 0, (0, 2), "V")
        wq("m", 0, 0)
        th(1, 1, 1)
        wq("p", 0, 0)
        th(1, 1, 2)
        hg(1, 0, "V")
        th(1, 1, 3)
        inter("p", 1, 0, (0, 2), "S")
        mS(0)
        inter("p", 1, 0, (2, 4), "S")
        hg(1, 1, "V")
        e(0)
        inter("m", 1, 0, (0, 2), "S")
        mS(1)
        hq(1, 0)
        e(1)
        wq("p", 1, 0)
        inter("m", 1, 0, (2, 4), "S")
        mS(2)
        hq(1, 1)
        mL(0)
        e(2)
        mL(1)
        wq("m", 1, 0)
        inter("s", 1, 1, (0, 2), "S")
        mS(3)
        ml(0)
        mM(0)
        ml(1)
        e(3)
        mM(1)
        ld(0)
        inter("s", 1, 1, (2, 4), "S")
        mS(4)
        ld(1)
        mL(2)
        d(0)
        pe(0, 0)
        mL(3)
        d(1)
        mM(2)
        wq("s", 1, 1)
        inter("m", 0, 1, (0, 2), "S")
        mM(3)
        s1(0, 0, "G")
        d(2)
        mR(0)
        d(3)
        inter("m", 0, 1, (2, 4), "S")
        ml(2)
        z(0, "G")
        mR(1)
        ml(3)
        inter("m", 1, 1, (0, 2), "S")
        ld(2)
        mM(4)
        ld(3)
        inter("m", 1, 1, (2, 4), "S")
        mL(4)
        d(4)
        z(1, "G")
        mL(5)
        ml(4)
        mM(5)
        pe(1, 0)
        ml(5)
        mM(6)
        ld(4)
        e(4)
        sq(0)
        ld(5)
        s2(0, 0, "G")
        mL(6)
        d(5)
        mL(7)
        s1(1, 0, "G")
        pe(2, 0)
        q(0)
        mS(5)
        q(1)
        mM(7)
        e(5)
        wq("m", 0, 1)
        mR(2)
        sq(1)
        wq("m", 1, 1)
        mS(6)
        mqr(0)
        z(2, "G")
        inter("p", 0, 1, (0, 2), "S")
        mR(3)
        q(2)
        e(6)
        q(3)
        inter("p", 0, 1, (2, 4), "S")
        mR(4)
        ml(6)
        qd(0, "G")
        mqr(1)
        sq(2)
        mS(7)
        mR(5)
        e(7)
        ml(7)
        inter("p", 1, 1, (0, 2), "S")
        q(4)
        mS(8)
        fd(0, "G")
        q(5)
        mR(6)
        pe(0, 1)
        d(6)
        s2(1, 0, "G")
        d(7)
        mM(8)
        e(8)
        s1(2, 0, "G")
        mqr(2)
        mM(9)
        inter("p", 1, 1, (2, 4), "S")
        mS(9)
        qd(1, "V")
        mR(7)
        e(9)
        wq("p", 0, 1)
        mS(10)
        pe(1, 1)
        qd(2, "G")
        d(8)
        d(9)
        tsum(1, 1)
        wq("p", 1, 1)
        pe(2, 1)
        z(3, "V")
        mM(10)
        cp(1)
        mM(11)
        z(4, "G")
        d(10)
        e(10)
        tsum(2, 1)
        d(11)
        sq(3)
        q(6)
        s2(2, 0, "G")
        q(7)
        sq(4)
        mS(11)
        s1(0, 1, "V")
        mR(8)
        cp(2)
        mqr(3)
        e(11)
        z(5, "G")
        mS(12)
        ld(6)
        mR(9)
        e(12)
        ld(7)
        q(8)
        pe(3, 0)
        mL(8)
        q(9)
        mL(9)
        qd(3, "G")
        ml(8)
        sq(5)
        mS(13)
        mqr(4)
        mM(12)
        e(13)
        mM(13)
        ld(8)
        mS(14)
        pe(3, 1)
        s2(0, 1, "V")
        mR(10)
        qd(4, "V")
        e(14)
        mL(10)
        s1(3, 0, "G")
        q(10)
        pe(4, 1)
        tsum(3, 1)
        d(12)
        d(13)
        s2(3, 0, "G")
        ml(9)
        z(6, "G")
        ml(10)
        mS(15)
        ld(9)
        cp(3)
        mR(11)
        ld(10)
        pe(4, 0)
        fd(1, "V")
        mL(11)
        e(15)
        s1(4, 0, "G")
        q(11)
        mL(12)
        sq(6)
        mM(14)
        ml(11)
        mM(15)
        mqr(5)
        s2(4, 0, "G")
        mR(12)
        ld(11)
        qd(5, "G")
        mR(13)
        q(12)
        pe(5, 0)
        d(14)
        mL(13)
        q(13)
        tsum(5, 0)
        d(15)
        fd(2, "G")
        pe(5, 1)
        ml(12)
        ml(13)
        z(7, "G")
        ld(12)
        ld(13)
        tsum(5, 1)
        pe(6, 0)
        s1(4, 1, "V")
        sq(7)
        mqa(6)
        s2(4, 1, "V")
        mL(14)
        cp(5)
        mqb(6)
        mL(15)
        s1(6, 0, "G")
        ml(14)
        ln(0)
        mR(14)
        ml(15)
        qd(6, "G")
        ld(14)
        mR(15)
        q(14)
        ld(15)
        ln(1)
        q(15)
        t1(0, "V")
        pe(7, 0)
        s2(6, 0, "G")
        mqr(7)
        o(0)
        qd(7, "V")
        pe(6, 1)
        s1(7, 0, "V")
        ob(0, "V")
        pe(7, 1)
        tsum(6, 1)
        t1(1, "V")
        oq(0)
        o(1)
        ln(2)
        fd(3, "V")
        ob(1, "V")
        s2(7, 0, "V")
        oq(1)
        s1(7, 1, "V")
        cp(6)
        t1(2, "V")
        la(3)
        s2(7, 1, "V")
        o(2)
        ln(3)
        t1(3, "V")
        ob(2, "S")
        oa(3)
        oq(2)
        o(3)
        ob(3, "V")
        oq(3)
